import numpy as np, ml_dtypes
CORES = [2,3,42,43,82,83,122,123]
N = 8
import mx_ref
BF = ml_dtypes.bfloat16
def entries(a):
    return np.ascontiguousarray(a.T).reshape(-1)
def table(e):
    return np.ascontiguousarray(np.reshape(e, (-1, 16)).T).astype(np.int32)
def f(rng, *shape):
    return mx_ref.flush((rng.standard_normal(shape, dtype=np.float32) * np.exp2(rng.integers(-2, 3, shape[:-1] + (1,)))).astype(BF))
def wide(rng, *shape, cols=0):
    v = rng.standard_normal(shape, dtype=np.float32) * np.exp2(rng.integers(-12, 13, shape)).astype(np.float32)
    if cols: v *= np.repeat(np.exp2(rng.integers(-cols, cols + 1, shape[:-2] + (1, shape[-1] // 4))) * (rng.random(shape[:-2] + (1, shape[-1] // 4)) > 0.0625), 4, axis=-1).astype(np.float32)
    return mx_ref.flush(v.astype(BF))
R, P, MOST = 5, 64, 5
def lists(rng, plan, tie=False):
    v = rng.integers(0, 1001, (N, R, P))
    hold = np.arange(P).reshape(N, 8)
    for t in range(R):
        for a in range(t % 2, N - 1, 2):
            A, B, go = v[a, t], v[a + 1, t], set(int(k) for k in plan(t, a))
            for k in range(8):
                p, q = int(hold[a, k]), int(hold[a + 1, k])
                if tie:
                    A[[p, q]] = rng.integers(300, 701, 2)
                    B[[p, q]] = A[[p, q]] + rng.integers(-200, 201)
                    if k in go: A[q] += 1
                else:
                    while A[q] + B[p] == A[p] + B[q]:
                        A[[p, q]] = rng.integers(0, 1001, 2)
                        B[[p, q]] = rng.integers(0, 1001, 2)
                    if (A[q] + B[p] > A[p] + B[q]) != (k in go):
                        A[[p, q]] = A[[q, p]]
                        B[[p, q]] = B[[q, p]]
                if k in go: hold[a, k], hold[a + 1, k] = q, p
    return {"dm": np.stack([table(e.reshape(-1)) for e in v])}
def setup_inputs(rng):
    return {"x": f(rng, N, 128, 512 * R), "w": f(rng, N, 128, 1024), **lists(rng, lambda t, a: rng.permutation(8)[:rng.integers(0, MOST + 1)])}
def setup_inputs_back(rng):
    go = rng.permutation(8)[:MOST]
    return {**setup_inputs(rng), **lists(rng, lambda t, a: [] if t % 2 else go)}
def setup_inputs_carry(rng):
    d = setup_inputs(rng)
    go = rng.permutation(8)[:MOST]
    c = rng.permutation(np.repeat([-5, 5], 4))
    e = np.where(np.arange(N)[:, None] % 2 == 0, c, -c)
    s = np.exp2(e).astype(np.float32)[:, None, :, None]
    d["w"] = mx_ref.flush((d["w"].astype(np.float32).reshape(N, 128, 8, 128) * s).reshape(N, 128, 1024).astype(BF))
    return {**d, **lists(rng, lambda t, a: go)}
def setup_inputs_equal(rng):
    return {**setup_inputs(rng), **lists(rng, lambda t, a: rng.permutation(8)[:MOST], tie=True)}
def setup_inputs_turn(rng):
    go = rng.permutation(8)
    return {**setup_inputs(rng), **lists(rng, lambda t, a: go[:MOST] if t < 2 else go[8 - MOST:])}
def setup_inputs_spread(rng):
    d = setup_inputs(rng); d["x"] = wide(rng, N, 128, 512 * R, cols=6); return d
def rounds(dm):
    v = np.stack([entries(e) for e in dm]).reshape(N, R, P)
    hold = np.arange(P).reshape(N, 8)
    held, most = [], 0
    for t in range(R):
        for a in range(t % 2, N - 1, 2):
            n = 0
            for k in range(8):
                p, q = int(hold[a, k]), int(hold[a + 1, k])
                if v[a, t, q] + v[a + 1, t, p] > v[a, t, p] + v[a + 1, t, q]:
                    hold[a, k], hold[a + 1, k] = q, p
                    n += 1
            most = max(most, n)
        held.append(np.array(hold))
    return held, most
def check_inputs(d):
    for n in ("x", "w"):
        m = np.abs(d[n].astype(np.float32))
        if not np.all((m == 0) | ((m >= 2.0 ** -30) & (m <= 2.0 ** 30))): return [n]
    if d["dm"].min() < 0 or d["dm"].max() > 1000: return ["dm"]
    return ["more than MOST slots change at a pair in a round"] if rounds(d["dm"])[1] > MOST else []
def reference(x, w, dm):
    held = rounds(dm)[0]
    y = np.zeros((N, 128, 256 * R), np.float32)
    for t in range(R):
        for r in range(N):
            X = mx_ref.quantize(np.ascontiguousarray(x[r][:, 512 * t:512 * t + 512]))
            for h in range(2):
                S = np.concatenate([w[p >> 3][:, 128 * (p & 7):128 * (p & 7) + 128] for p in held[t][r, 4 * h:4 * h + 4]], axis=1)
                y[r][:, 256 * t + 128 * h:256 * t + 128 * h + 128] = mx_ref.matmul(mx_ref.quantize(S), X)
    return {"y": y}

@@ -1,0 +1,381 @@
+from concourse.bass import DstId, RemoteDMATransfer
+from concourse.mybir import dt, AluOpType as Op, ActivationFunctionType as Act
+
+C8 = "float8_e4m3fn_x4"
+SCRATCH = {
+    "d3": ("dram", [128, 3], "int32"),
+    "wt": ("sbuf", [128, 1024], "bfloat16"),
+    "xt": ("sbuf", [128, 2560], "bfloat16"),
+    "xq": ("sbuf", [128, 640], C8), "xs": ("sbuf", [128, 640], "uint8"),
+    "hb": ("sbuf", [128, 1024], C8), "hbs": ("sbuf", [128, 1024], "uint8"),
+    "win": ("sbuf", [128, 1536], C8), "wins": ("sbuf", [128, 1536], "uint8"),
+    "sr": ("sbuf", [128, 256], C8), "srs": ("sbuf", [128, 256], "uint8"),
+    "su": ("sbuf", [128, 256], C8), "sus": ("sbuf", [128, 256], "uint8"),
+    "pk": ("sbuf", [128, 1280], C8), "pks": ("sbuf", [128, 1280], "uint8"),
+    "se0": ("sbuf", [128, 6, 16], "int32"), "se1": ("sbuf", [128, 6, 16], "int32"),
+    "so0": ("sbuf", [128, 6, 16], "int32"), "so1": ("sbuf", [128, 6, 16], "int32"),
+    "sta": ("sbuf", [128, 68], "float32"), "stb": ("sbuf", [128, 68], "float32"),
+    "e0": ("sbuf", [128, 32], "float32"),
+    "dd": ("sbuf", [128, 64], "float32"), "cd": ("sbuf", [128, 64], "float32"),
+    "ce": ("sbuf", [128, 8], "float32"), "co": ("sbuf", [128, 8], "float32"),
+    "wk": ("sbuf", [128, 32], "float32"),
+    "li": ("sbuf", [128, 8], "float32"), "pp": ("sbuf", [128, 2], "float32"),
+    "pi": ("sbuf", [128, 4], "int32"), "pj": ("sbuf", [128, 4], "int32"), "p3": ("sbuf", [128, 4], "int32"),
+    "of": ("sbuf", [128, 4], "uint16"),
+    "tt": ("sbuf", [128, 64], "float32"), "tr": ("sbuf", [128, 64], "float32"),
+    "bj": ("sbuf", [128, 16], "float32"), "jl": ("sbuf", [128, 32], "uint16"),
+    "tf": ("sbuf", [128, 160], "float32"), "bf": ("sbuf", [128, 40], "float32"), "lu": ("sbuf", [128, 80], "uint16"),
+    "ys": ("sbuf", [128, 1280], "float32"),
+    "acc": ("psum", [128, 4096], "float32"),
+}
+for _j in range(8):
+    SCRATCH["ld%d" % _j] = ("dram", [128, 3], "int32")
+SEMAPHORES = ["sD", "wld", "xld", "own", "lp", "lh", "lo", "sP", "sH", "sO", "bp", "bo", "x1", "x2", "cw",
+              "vs", "gs", "ss", "ps", "st", "ls"]
+
+TI = [0, 1, 2, 4, 5]
+COL = {1: 48, 2: 32, 3: 20, 4: 4}
+SIZE = [64, 48, 32, 32, 16]
+
+
+def rank_program(g, core, T, topo):
+    r = T.rank_of(core)
+    if r is None:
+        return
+    S = T.sem
+    v, sc, sy, te = g.vector, g.scalar, g.sync, g.tensor
+    h = r // 4
+    mid = r in (2, 3, 4, 5)
+    bound = r == 3 + h
+    lo = r - 4 * h
+    cv, cg, cs, cp, cl, cst = [0], [0], [0], [0], [0], [0]
+
+    def V(i):
+        i.then_inc(S.vs, 1)
+        cv[0] += 1
+        return cv[0]
+
+    def vw():
+        v.wait_ge(S.vs, cv[0])
+
+    def G(i):
+        i.then_inc(S.gs, 1)
+        cg[0] += 1
+        return cg[0]
+
+    def A(i):
+        i.then_inc(S.ss, 1)
+        cs[0] += 1
+        return cs[0]
+
+    def dst(k):
+        a = topo.addr(T.cores[k])
+        return DstId(rid=a[0], pnc=a[1])
+
+    def bits(es):
+        return sum(1 << e for e in es)
+
+    partner = r ^ 1
+    far = [k for k in range(4 * h, 4 * h + 4) if k // 2 != r // 2]
+    other = [k for k in range(8) if k // 4 != h]
+    off = topo.engines(core, T.cores[far[0]])
+    on = [e for e in topo.engines(core, T.cores[partner]) if e not in off]
+
+    sy.dma_start(T.d3[0:64, :], T.dm[:, 0:12]).then_inc(S.sD, 16)
+    sc.dma_start(T.d3[64:128, :], T.dm[:, 8:20]).then_inc(S.sD, 16)
+    sy.dma_start(T.wt[:], T.w[:]).then_inc(S.wld, 16)
+
+    def home(j, s, hh):
+        return T["so%d" % s if j % 2 else "se%d" % s][0:8, 3 * hh:3 * hh + 3, 4 * (j // 2):4 * (j // 2) + 4]
+
+    for s in range(2):
+        for hh in range(2):
+            sc.dma_start(home(r, s, hh), T.dm[8 * s:8 * s + 8, 8 * hh:8 * hh + 12]).then_inc(S.own, 16)
+    sy.dma_start(T.xt[:], T.x[:]).then_inc(S.xld, 16)
+
+    G(g.iota(T.pi[:], [[0, 4]], 0, 1))
+    fl = dict(allow_small_or_imprecise_dtypes=True)
+    G(g.iota(T.li[:, 0:2], [[512, 2]], 0, 32, **fl))
+    G(g.iota(T.li[:, 2:4], [[512, 2]], 256, 32, **fl))
+    G(g.iota(T.li[:, 4:6], [[256, 2]], 1024, 32, **fl))
+    G(g.iota(T.li[:, 6:7], [[1, 1]], 0 if h else 256, 32, **fl))
+    G(g.iota(T.li[:, 7:8], [[1, 1]], 256 if h else 512, 32, **fl))
+    nconst = cg[0]
+    for b in ("sta", "stb", "dd", "ce", "co", "tt"):
+        V(v.memset(T[b][:], 0.0))
+    v.wait_ge(S.gs, nconst)
+    V(v.tensor_scalar(T.pj[:], T.pi[:], 15, None, Op.bitwise_and))
+    V(v.tensor_scalar(T.p3[:], T.pi[:], 3, None, Op.bitwise_and))
+    vw()
+    V(v.tensor_copy(T.pp[:, 0:1], T.pj[:, 0:1]))
+    V(v.tensor_scalar(T.pp[:, 1:2], T.pj[:, 0:1], 16.0, None, Op.add))
+    V(v.tensor_copy(T.of[:], T.p3[:]))
+
+    g.wait_ge(S.sD, 32)
+    ld = T["ld%d" % r]
+
+    def lists(ks, e, sem):
+        return RemoteDMATransfer(dst_ids=[dst(k) for k in ks], dma_engine_mask=1 << e, remote_sem=sem,
+                                 srcs=[T.d3[:]], dsts=[ld[:] for k in ks])
+
+    g.remote_dma_fused([lists([partner], on[0], S.lp), lists(far, off[0], S.lh), lists(other, off[2], S.lo)],
+                       local_sem=S.ls)
+    cl[0] += 3
+
+    c0 = 256 * lo
+    v.wait_ge(S.wld, 16)
+    nq = V(v.quantize_mx(T.hb[:, c0:c0 + 256], T.hbs[:, c0:c0 + 256], T.wt[:]))
+    if not mid:
+        V(v.quantize_mx(T.win[:, c0:c0 + 256], T.wins[:, c0:c0 + 256], T.wt[:]))
+    g.wait_ge(S.vs, nq)
+
+    def dbuf(k, plane):
+        b = T[("hb" if k in (2, 3, 4, 5) else "win") + ("s" if plane else "")]
+        return b[:, c0:c0 + 256] if plane else b[:, c0:c0 + 256].bitcast(dt.uint8)
+
+    for plane in (False, True):
+        src = T.hbs[:, c0:c0 + 256] if plane else T.hb[:, c0:c0 + 256].bitcast(dt.uint8)
+        g.remote_dma_fused([
+            RemoteDMATransfer(dst_ids=[dst(partner)], dma_engine_mask=bits(on), remote_sem=S.bp,
+                              srcs=[src], dsts=[dbuf(partner, plane)]),
+            RemoteDMATransfer(dst_ids=[dst(k) for k in far], dma_engine_mask=bits(off), remote_sem=S.bo,
+                              srcs=[src], dsts=[dbuf(k, plane) for k in far])], local_sem=S.ls)
+        cl[0] += len(on) + len(off)
+
+    v.wait_ge(S.xld, 16)
+    V(v.quantize_mx(T.xq[:, 0:512], T.xs[:, 0:512], T.xt[:, 0:2048]))
+    nx = V(v.quantize_mx(T.xq[:, 512:640], T.xs[:, 512:640], T.xt[:, 2048:2560]))
+
+    def bring(q, j, s, hh, sem):
+        a = 64 * hh + 32 * s
+        q.dma_start(home(j, s, hh), T["ld%d" % j][a:a + 32, :]).then_inc(sem, 16)
+
+    for s, q in ((0, sy), (1, sc)):
+        q.wait_ge(S.lp, 1)
+        bring(q, partner, s, 0, S.sP)
+        q.wait_ge(S.lh, 2)
+        for j in far:
+            bring(q, j, s, 0, S.sH)
+        q.wait_ge(S.lo, 4)
+        for j in other:
+            bring(q, j, s, 0, S.sO)
+        for j in other + far + [partner]:
+            bring(q, j, s, 1, S.sO)
+    tot_o = 16 * 2 * (4 + 7)
+
+    if mid:
+        sy.wait_ge(S.vs, nq)
+        sy.wait_ge(S.bp, 16)
+        sy.wait_ge(S.bo, 32)
+        sy.dma_start(T.win[:, 0:1024].bitcast(dt.uint8), T.hb[:].bitcast(dt.uint8)).then_inc(S.cw, 16)
+        sy.dma_start(T.wins[:, 0:1024], T.hbs[:]).then_inc(S.cw, 16)
+
+    if mid:
+        W = T.wk
+        v.wait_ge(S.own, 64)
+        v.wait_ge(S.sP, 32)
+        sgn = 256.0 if h else -256.0
+        w0 = 0 if h else 512
+        jobs = []
+
+        def row(i):
+            vw()
+            n = V(v.transpose(T.tr[0:32, 32 * i:32 * i + 32], T.tt[0:32, 32 * i:32 * i + 32]))
+            g.wait_ge(S.vs, n)
+            return G(g.partition_broadcast(T.bj[0:128, 8 * i:8 * i + 8], T.tr[0:1, 32 * i:32 * i + 8], 128))
+
+        if bound:
+            a = 5 * (r // 2)
+            V(v.tensor_tensor(W[0:8, 0:1], T.se0[0:8, 0, a:a + 1], T.so0[0:8, 0, a:a + 1], Op.subtract))
+            V(v.tensor_tensor(W[0:8, 1:2], T.se1[0:8, 0, a:a + 1], T.so1[0:8, 0, a:a + 1], Op.subtract))
+            vw()
+            V(v.tensor_scalar(W[0:8, 2:3], W[0:8, 1:2], W[0:8, 0:1], sgn, Op.is_gt, Op.mult))
+            vw()
+            V(v.tensor_scalar(T.tt[0:8, 0:1], W[0:8, 2:3], T.li[0:8, 6:7], None, Op.add))
+            to = [4, 5, 6] if h == 0 else [3, 2, 1]
+            jobs.append((0, row(0), "sr", w0, w0 + 512, to, 1024, "x1"))
+        else:
+            v.wait_ge(S.sH, 64)
+            n = 2 * h
+            a, near = 5 * n, 1 - h
+            V(v.tensor_tensor(W[0:8, 0:2], T.se0[0:8, 0, a:a + 6:5], T.so0[0:8, 0, a:a + 6:5], Op.subtract))
+            V(v.tensor_tensor(W[0:8, 2:4], T.se1[0:8, 0, a:a + 6:5], T.so1[0:8, 0, a:a + 6:5], Op.subtract))
+            b = 4 * n + n
+            V(v.tensor_tensor(W[0:8, 8:10], T.so0[0:8, 1, b:b + 2], T.se0[0:8, 1, b + 4:b + 6], Op.subtract))
+            V(v.tensor_tensor(W[0:8, 10:12], T.so1[0:8, 1, b:b + 2], T.se1[0:8, 1, b + 4:b + 6], Op.subtract))
+            vw()
+            V(v.tensor_tensor(W[0:8, 4:6], W[0:8, 2:4], W[0:8, 0:2], Op.is_gt))
+            V(v.tensor_tensor(W[0:8, 12:13], W[0:8, 8:9], W[0:8, 10:11], Op.subtract))
+            V(v.tensor_tensor(W[0:8, 13:14], W[0:8, 11:12], W[0:8, 9:10], Op.subtract))
+            vw()
+            V(v.tensor_scalar(T.tt[0:8, 0:1], W[0:8, 4 + near:5 + near], sgn, T.li[0:8, 6:7], Op.mult, Op.add))
+            k0 = row(0)
+            V(v.tensor_scalar(W[0:8, 14:15], W[0:8, 12:13], W[0:8, 4:5], W[0:8, 10:11], Op.mult, Op.add))
+            V(v.tensor_scalar(W[0:8, 15:16], W[0:8, 13:14], W[0:8, 5:6], W[0:8, 9:10], Op.mult, Op.add))
+            V(v.tensor_tensor(W[0:8, 16:17], W[0:8, 4:5], W[0:8, 5:6], Op.add))
+            i = 4 if h else 5
+            V(v.tensor_scalar(W[0:8, 18:19], W[0:8, i:i + 1], -sgn, T.li[0:8, 7:8], Op.mult, Op.add))
+            vw()
+            V(v.tensor_scalar(W[0:8, 17:18], W[0:8, 16:17], sgn, sgn, Op.mult, Op.add))
+            vw()
+            V(v.tensor_scalar(W[0:8, 19:20], W[0:8, 15:16], W[0:8, 14:15], W[0:8, 17:18], Op.is_gt, Op.mult))
+            vw()
+            V(v.tensor_scalar(T.tt[0:8, 32:33], W[0:8, 19:20], W[0:8, 18:19], None, Op.add))
+            k1 = row(1)
+            jobs.append((0, k0, "sr", w0, w0 + 512, [7] if h == 0 else [0], 1024, "x1"))
+            jobs.append((1, k1, "su", 0, 1024, [4, 5] if h == 0 else [3, 2], 1280, "x2"))
+        for i, k, b, wa, wb, to, col, sem in jobs:
+            v.wait_ge(S.gs, k)
+            o = 16 * i
+            V(v.tensor_scalar(T.jl[:, o:o + 16:2], T.bj[:, 8 * i:8 * i + 8], T.pp[:, 0:1], None, Op.add))
+            nl = V(v.tensor_scalar(T.jl[:, o + 1:o + 16:2], T.bj[:, 8 * i:8 * i + 8], T.pp[:, 1:2], None, Op.add))
+            vw()
+            for q in (v, sc):
+                q.wait_ge(S.bp, 16)
+                if i == 1:
+                    q.wait_ge(S.bo, 32)
+            n1 = V(v.tensor_copy(T[b][:].bitcast(dt.uint32), T.hb[:, wa:wb].bitcast(dt.uint32).indirect(T.jl[:, o:o + 16])))
+            sc.wait_ge(S.vs, nl)
+            n2 = A(sc.activation(T[b + "s"][:], T.hbs[:, wa:wb].indirect(T.jl[:, o:o + 16]), Act.Copy))
+            for plane in (False, True):
+                if plane:
+                    g.wait_ge(S.ss, n2)
+                    src, ds = T[b + "s"][:], [T.wins[:, col:col + 256] for k2 in to]
+                else:
+                    g.wait_ge(S.vs, n1)
+                    src, ds = T[b][:].bitcast(dt.uint8), [T.win[:, col:col + 256].bitcast(dt.uint8) for k2 in to]
+                g.remote_dma_fused([RemoteDMATransfer(dst_ids=[dst(k2) for k2 in to], dma_engine_mask=bits(off),
+                                                      remote_sem=S[sem], srcs=[src], dsts=ds)], local_sem=S.ls)
+                cl[0] += len(off)
+
+    v.wait_ge(S.own, 64)
+    v.wait_ge(S.sP, 32)
+    v.wait_ge(S.sH, 64)
+    v.wait_ge(S.sO, tot_o)
+    st = (T.sta, T.stb)
+    for s in range(2):
+        se, so = T["se%d" % s], T["so%d" % s]
+        V(v.tensor_tensor(T.e0[0:8, 16 * s:16 * s + 16], se[0:8, 0, :], so[0:8, 0, :], Op.subtract))
+        V(v.tensor_copy(st[s][0:8, 2 * h:2 * h + 2], T.li[0:8, 2 * s:2 * s + 2]))
+        for t in (1, 2, 3, 4):
+            c, i = COL[t], TI[t]
+            if t % 2 == 0:
+                V(v.tensor_tensor(st[s][0:8, c:c + 16], se[0:8, i, :], so[0:8, i, :], Op.subtract))
+            else:
+                V(v.tensor_tensor(st[s][0:8, c:c + 12], so[0:8, i, 0:12], se[0:8, i, 4:16], Op.subtract))
+    level = [0] * 8
+    need = []
+    rows = []
+    for t in range(5):
+        n = SIZE[t]
+        odd = t % 2
+        vw()
+        if not odd:
+            a, b = T.sta[0:8, 0:n], T.stb[0:8, 0:n]
+            if t == 0:
+                ea, eb = T.e0[0:8, 0:16:5], T.e0[0:8, 16:32:5]
+            else:
+                c = COL[t]
+                ea, eb = T.sta[0:8, c:c + 16:5], T.stb[0:8, c:c + 16:5]
+            cc, V0 = T.ce, 4
+        else:
+            a, b = T.stb[0:8, 0:n], T.sta[0:8, 1:n + 1]
+            c = COL[t]
+            ea, eb = T.stb[0:8, c:c + 11:5], T.sta[0:8, c + 1:c + 12:5]
+            cc, V0 = T.co, 3
+        V(v.tensor_tensor(cc[0:8, 0:V0], eb, ea, Op.is_gt))
+        V(v.tensor_tensor(T.dd[0:8, 0:n], b, a, Op.subtract))
+        vw()
+        V(v.tensor_tensor(T.cd[:, 0:n], cc[:, 0:8].indirect(T.of[:, 0:n // 16]), T.dd[:, 0:n], Op.mult))
+        vw()
+        V(v.tensor_tensor(a, a, T.cd[0:8, 0:n], Op.add))
+        V(v.tensor_tensor(b, b, T.cd[0:8, 0:n], Op.subtract))
+        for k in range(odd, 7, 2):
+            level[k] = level[k + 1] = max(level[k], level[k + 1])
+        if t < 2:
+            pos = (4 + t) if h == 0 else (3 - t)
+            vw()
+            V(v.tensor_copy(st[pos % 2][0:8, pos // 2:pos // 2 + 1], T.li[0:8, 4 + t:5 + t]))
+            level[pos] = 1 + t
+        need.append(level[r])
+        vw()
+        k = V(v.transpose(T.tf[0:32, 32 * t:32 * t + 32], st[r % 2][0:32, r // 2:r // 2 + 32]))
+        g.wait_ge(S.vs, k)
+        rows.append(G(g.partition_broadcast(T.bf[0:128, 8 * t:8 * t + 8], T.tf[0:1, 32 * t:32 * t + 8], 128)))
+
+    copied = {}
+    fetched = {}
+
+    def ready(q, lv):
+        if mid:
+            q.wait_ge(S.cw, 32)
+        else:
+            q.wait_ge(S.vs, nq + 1)
+            q.wait_ge(S.bp, 16)
+            q.wait_ge(S.bo, 32)
+        if lv >= 1:
+            q.wait_ge(S.x1, 16)
+        if lv >= 2:
+            q.wait_ge(S.x2, 16)
+
+    nlist = []
+    for t in range(5):
+        v.wait_ge(S.gs, rows[t])
+        V(v.tensor_scalar(T.lu[:, 16 * t:16 * t + 16:2], T.bf[:, 8 * t:8 * t + 8], T.pp[:, 0:1], None, Op.add))
+        nlist.append(V(v.tensor_scalar(T.lu[:, 16 * t + 1:16 * t + 16:2], T.bf[:, 8 * t:8 * t + 8], T.pp[:, 1:2], None, Op.add)))
+
+    def out(t):
+        o = 256 * t
+        e = [512 * ((2 * t + k) % 8) for k in range(2)]
+        v.wait_ge(S.ps, 2 * t + 1)
+        n1 = V(v.tensor_copy(T.ys[:, o:o + 128], T.acc[:, e[0]:e[0] + 128]))
+        sc.wait_ge(S.ps, 2 * t + 2)
+        n2 = A(sc.activation(T.ys[:, o + 128:o + 256], T.acc[:, e[1]:e[1] + 128], Act.Copy))
+        copied[t] = (n1, n2)
+        sy.wait_ge(S.vs, n1)
+        if t < 4:
+            sy.wait_ge(S.ss, n2)
+            sy.dma_start(T.y[:, o:o + 256], T.ys[:, o:o + 256]).then_inc(S.st, 16)
+            cst[0] += 16
+        else:
+            sy.dma_start(T.y[:, o:o + 128], T.ys[:, o:o + 128]).then_inc(S.st, 16)
+            sc.wait_ge(S.ss, n2)
+            sc.dma_start(T.y[:, o + 128:o + 256], T.ys[:, o + 128:o + 256]).then_inc(S.st, 16)
+            cst[0] += 32
+
+    for t in range(5):
+        lv = max(need[t], 0)
+        w = 1024 + 256 * lv
+        o = 256 * t
+        fs = T.lu[:, 16 * t:16 * t + 16]
+        vw()
+        ready(v, lv)
+        n1 = V(v.tensor_copy(T.pk[:, o:o + 256].bitcast(dt.uint32), T.win[:, 0:w].bitcast(dt.uint32).indirect(fs)))
+        sc.wait_ge(S.vs, nlist[t])
+        ready(sc, lv)
+        n2 = A(sc.activation(T.pks[:, o:o + 256], T.wins[:, 0:w].indirect(fs), Act.Copy))
+        te.wait_ge(S.vs, max(n1, nx))
+        te.wait_ge(S.ss, n2)
+        if t == 4:
+            te.wait_ge(S.vs, copied[0][0])
+            te.wait_ge(S.ss, copied[0][1])
+        for k in range(2):
+            e = 512 * ((2 * t + k) % 8)
+            c = o + 128 * k
+            te.matmul_mx(T.acc[:, e:e + 128], T.pk[:, c:c + 128], T.pks[:, c:c + 128],
+                         T.xq[:, 128 * t:128 * t + 128], T.xs[:, 128 * t:128 * t + 128], True, True).then_inc(S.ps, 1)
+        if t > 0:
+            out(t - 1)
+    out(4)
+
+    if mid:
+        v.wait_ge(S.x1, 16)
+        v.wait_ge(S.x2, 16)
+    else:
+        v.wait_ge(S.x1, 16)
+    vw()
+    sc.wait_ge(S.ss, cs[0])
+    te.wait_ge(S.ps, 10)
+    sy.wait_ge(S.st, cst[0])
+    g.wait_ge(S.gs, cg[0])
+    g.wait_ge(S.ls, cl[0])

@@ -8,12 +8,15 @@ SCRATCH = {
     "xt": ("sbuf", [128, 2560], "bfloat16"),
     "xq": ("sbuf", [128, 640], C8), "xs": ("sbuf", [128, 640], "uint8"),
     "hb": ("sbuf", [128, 1024], C8), "hbs": ("sbuf", [128, 1024], "uint8"),
+    "fw": ("sbuf", [128, 256], C8), "fws": ("sbuf", [128, 256], "uint8"),
     "win": ("sbuf", [128, 1536], C8), "wins": ("sbuf", [128, 1536], "uint8"),
     "sr": ("sbuf", [128, 256], C8), "srs": ("sbuf", [128, 256], "uint8"),
     "su": ("sbuf", [128, 256], C8), "sus": ("sbuf", [128, 256], "uint8"),
     "pk": ("sbuf", [128, 1280], C8), "pks": ("sbuf", [128, 1280], "uint8"),
-    "se0": ("sbuf", [128, 6, 16], "int32"), "se1": ("sbuf", [128, 6, 16], "int32"),
-    "so0": ("sbuf", [128, 6, 16], "int32"), "so1": ("sbuf", [128, 6, 16], "int32"),
+    "se0": ("sbuf", [128, 2, 4, 12], "int32"), "se1": ("sbuf", [128, 2, 4, 12], "int32"),
+    "so0": ("sbuf", [128, 2, 4, 12], "int32"), "so1": ("sbuf", [128, 2, 4, 12], "int32"),
+    "cr": ("sbuf", [128, 4], "float32"),
+    "cp": ("sbuf", [128, 1], "float32"), "ck": ("sbuf", [128, 1], "float32"), "cx": ("sbuf", [128, 4], "float32"),
     "sta": ("sbuf", [128, 68], "float32"), "stb": ("sbuf", [128, 68], "float32"),
     "e0": ("sbuf", [128, 32], "float32"),
     "dd": ("sbuf", [128, 64], "float32"), "cd": ("sbuf", [128, 64], "float32"),
@@ -30,25 +33,58 @@ SCRATCH = {
 }
 for _j in range(8):
     SCRATCH["ld%d" % _j] = ("dram", [128, 3], "int32")
-SEMAPHORES = ["sD", "wld", "xld", "own", "lp", "lh", "lo", "sP", "sH", "sO", "bp", "bo", "x1", "x2", "cw",
+SEMAPHORES = ["sD", "wld", "xld", "own", "ow2", "lp", "lh", "lo", "kp", "kf", "sO", "bp", "bq", "bo", "x1", "x2", "cw",
               "vs", "gs", "ss", "ps", "st", "ls"]
 
-TI = [0, 1, 2, 4, 5]
+TI = [(0, 0), (0, 4), (0, 8), (1, 4), (1, 8)]
 COL = {1: 48, 2: 32, 3: 20, 4: 4}
 SIZE = [64, 48, 32, 32, 16]
+MID = (2, 3, 4, 5)
 
 
 def rank_program(g, core, T, topo):
+    S = T.sem
+
+    def dst(c):
+        a = topo.addr(c)
+        return DstId(rid=a[0], pnc=a[1])
+
+    def bits(es):
+        return sum(1 << e for e in es)
+
+    def away(r):
+        h = r // 4
+        return [k for k in ((2, 3, 0, 1) if h == 0 else (5, 4, 7, 6)) if k // 2 != r // 2]
+
+    def helper(r):
+        c = T.cores[r]
+        return [k for k in topo.cores_of(c) if T.rank_of(k) is None and topo.die(k) != topo.die(c)
+                and topo.may_write(k, T.cores[away(r)[1]])][r % 2]
+
+    def half_buf(r, k, plane):
+        c0 = 256 * (r % 4)
+        b = T[("hb" if k in MID else "win") + ("s" if plane else "")]
+        return b[:, c0:c0 + 256] if plane else b[:, c0:c0 + 256].bitcast(dt.uint8)
+
     r = T.rank_of(core)
     if r is None:
+        for k in range(8):
+            if helper(k) == core:
+                to = away(k)[1]
+                es = topo.engines(core, T.cores[to])
+                a = topo.addr(T.cores[to])
+                for sem, plane in ((S.bp, False), (S.bq, True)):
+                    g.wait_ge(sem, 8)
+                    g.remote_dma(half_buf(k, to, plane), T.fws[:] if plane else T.fw[:].bitcast(dt.uint8),
+                                 S.bo, S.ls, a[1], a[0], bits(es))
+                g.wait_ge(S.ls, 2 * len(es))
         return
-    S = T.sem
     v, sc, sy, te = g.vector, g.scalar, g.sync, g.tensor
     h = r // 4
-    mid = r in (2, 3, 4, 5)
+    mid = r in MID
     bound = r == 3 + h
     lo = r - 4 * h
-    cv, cg, cs, cp, cl, cst = [0], [0], [0], [0], [0], [0]
+    cv, cg, cs, cl, cst = [0], [0], [0], [0], [0]
 
     def V(i):
         i.then_inc(S.vs, 1)
@@ -68,29 +104,23 @@ def rank_program(g, core, T, topo):
         cs[0] += 1
         return cs[0]
 
-    def dst(k):
-        a = topo.addr(T.cores[k])
-        return DstId(rid=a[0], pnc=a[1])
-
-    def bits(es):
-        return sum(1 << e for e in es)
-
     partner = r ^ 1
-    far = [k for k in range(4 * h, 4 * h + 4) if k // 2 != r // 2]
+    inner, outer, third = (2, 0, 1) if h == 0 else (5, 7, 6)
+    far = away(r)
     other = [k for k in range(8) if k // 4 != h]
     off = topo.engines(core, T.cores[far[0]])
     on = [e for e in topo.engines(core, T.cores[partner]) if e not in off]
 
+    def home(j, s, hh):
+        return T["so%d" % s if j % 2 else "se%d" % s][0:8, hh, j // 2, :]
+
     sy.dma_start(T.d3[0:64, :], T.dm[:, 0:12]).then_inc(S.sD, 16)
     sc.dma_start(T.d3[64:128, :], T.dm[:, 8:20]).then_inc(S.sD, 16)
-    sy.dma_start(T.wt[:], T.w[:]).then_inc(S.wld, 16)
-
-    def home(j, s, hh):
-        return T["so%d" % s if j % 2 else "se%d" % s][0:8, 3 * hh:3 * hh + 3, 4 * (j // 2):4 * (j // 2) + 4]
-
-    for s in range(2):
-        for hh in range(2):
-            sc.dma_start(home(r, s, hh), T.dm[8 * s:8 * s + 8, 8 * hh:8 * hh + 12]).then_inc(S.own, 16)
+    for hh in range(2):
+        for s, q in ((0, sy), (1, sc)):
+            q.dma_start(home(r, s, hh), T.dm[8 * s:8 * s + 8, 8 * hh:8 * hh + 12]).then_inc(S.ow2 if hh else S.own, 16)
+        if hh == 0:
+            sy.dma_start(T.wt[:], T.w[:]).then_inc(S.wld, 16)
     sy.dma_start(T.xt[:], T.x[:]).then_inc(S.xld, 16)
 
     G(g.iota(T.pi[:], [[0, 4]], 0, 1))
@@ -101,7 +131,7 @@ def rank_program(g, core, T, topo):
     G(g.iota(T.li[:, 6:7], [[1, 1]], 0 if h else 256, 32, **fl))
     G(g.iota(T.li[:, 7:8], [[1, 1]], 256 if h else 512, 32, **fl))
     nconst = cg[0]
-    for b in ("sta", "stb", "dd", "ce", "co", "tt"):
+    for b in ("cr", "sta", "stb", "dd", "ce", "co", "tt"):
         V(v.memset(T[b][:], 0.0))
     v.wait_ge(S.gs, nconst)
     V(v.tensor_scalar(T.pj[:], T.pi[:], 15, None, Op.bitwise_and))
@@ -115,12 +145,34 @@ def rank_program(g, core, T, topo):
     ld = T["ld%d" % r]
 
     def lists(ks, e, sem):
-        return RemoteDMATransfer(dst_ids=[dst(k) for k in ks], dma_engine_mask=1 << e, remote_sem=sem,
+        return RemoteDMATransfer(dst_ids=[dst(T.cores[k]) for k in ks], dma_engine_mask=1 << e, remote_sem=sem,
                                  srcs=[T.d3[:]], dsts=[ld[:] for k in ks])
 
     g.remote_dma_fused([lists([partner], on[0], S.lp), lists(far, off[0], S.lh), lists(other, off[2], S.lo)],
                        local_sem=S.ls)
     cl[0] += 3
+
+    m, n2 = r // 2, 2 * h
+    o0, o1 = (T.so0, T.so1) if r % 2 else (T.se0, T.se1)
+    v.wait_ge(S.own, 32)
+    vw()
+    V(v.tensor_tensor(T.cr[0:8, 0:1], o1[0:8, 0, m, m:m + 1], o0[0:8, 0, m, m:m + 1], Op.subtract))
+    c = 4 + n2
+    if r in (inner, third):
+        V(v.tensor_tensor(T.cr[0:8, 1:2], o0[0:8, 0, m, c:c + 1], o1[0:8, 0, m, c:c + 1], Op.subtract))
+        V(v.tensor_tensor(T.cr[0:8, 2:3], o0[0:8, 0, m, c + 1:c + 2], o1[0:8, 0, m, c:c + 1], Op.subtract))
+        V(v.tensor_tensor(T.cr[0:8, 3:4], o1[0:8, 0, m, c + 1:c + 2], o0[0:8, 0, m, c + 1:c + 2], Op.subtract))
+    g.wait_ge(S.vs, cv[0])
+    if mid:
+        to, es, sem, src, land = partner, on, S.kp, T.cr[:, 0:1], T.cp[:]
+    elif r == outer:
+        to, es, sem, src, land = inner, off, S.kf, T.cr[:, 0:1], T.ck[:]
+    else:
+        to, es, sem, src, land = inner, off, S.kf, T.cr[:], T.cx[:]
+    a = topo.addr(T.cores[to])
+    g.remote_dma(land, src, sem, S.ls, a[1], a[0], bits(es))
+    ncrit = len(es)
+    cl[0] += ncrit
 
     c0 = 256 * lo
     v.wait_ge(S.wld, 16)
@@ -128,52 +180,40 @@ def rank_program(g, core, T, topo):
     if not mid:
         V(v.quantize_mx(T.win[:, c0:c0 + 256], T.wins[:, c0:c0 + 256], T.wt[:]))
     g.wait_ge(S.vs, nq)
-
-    def dbuf(k, plane):
-        b = T[("hb" if k in (2, 3, 4, 5) else "win") + ("s" if plane else "")]
-        return b[:, c0:c0 + 256] if plane else b[:, c0:c0 + 256].bitcast(dt.uint8)
-
     for plane in (False, True):
         src = T.hbs[:, c0:c0 + 256] if plane else T.hb[:, c0:c0 + 256].bitcast(dt.uint8)
         g.remote_dma_fused([
-            RemoteDMATransfer(dst_ids=[dst(partner)], dma_engine_mask=bits(on), remote_sem=S.bp,
-                              srcs=[src], dsts=[dbuf(partner, plane)]),
-            RemoteDMATransfer(dst_ids=[dst(k) for k in far], dma_engine_mask=bits(off), remote_sem=S.bo,
-                              srcs=[src], dsts=[dbuf(k, plane) for k in far])], local_sem=S.ls)
+            RemoteDMATransfer(dst_ids=[dst(T.cores[partner]), dst(helper(r))], dma_engine_mask=bits(on),
+                              remote_sem=S.bq if plane else S.bp, srcs=[src],
+                              dsts=[half_buf(r, partner, plane), T.fws[:] if plane else T.fw[:].bitcast(dt.uint8)]),
+            RemoteDMATransfer(dst_ids=[dst(T.cores[far[0]])], dma_engine_mask=bits(off), remote_sem=S.bo,
+                              srcs=[src], dsts=[half_buf(r, far[0], plane)])], local_sem=S.ls)
         cl[0] += len(on) + len(off)
 
-    v.wait_ge(S.xld, 16)
-    V(v.quantize_mx(T.xq[:, 0:512], T.xs[:, 0:512], T.xt[:, 0:2048]))
-    nx = V(v.quantize_mx(T.xq[:, 512:640], T.xs[:, 512:640], T.xt[:, 2048:2560]))
-
-    def bring(q, j, s, hh, sem):
-        a = 64 * hh + 32 * s
-        q.dma_start(home(j, s, hh), T["ld%d" % j][a:a + 32, :]).then_inc(sem, 16)
-
     for s, q in ((0, sy), (1, sc)):
-        q.wait_ge(S.lp, 1)
-        bring(q, partner, s, 0, S.sP)
-        q.wait_ge(S.lh, 2)
-        for j in far:
-            bring(q, j, s, 0, S.sH)
-        q.wait_ge(S.lo, 4)
-        for j in other:
-            bring(q, j, s, 0, S.sO)
-        for j in other + far + [partner]:
-            bring(q, j, s, 1, S.sO)
-    tot_o = 16 * 2 * (4 + 7)
+        for sem, n, js in ((S.lp, 1, [partner]), (S.lh, 2, far), (S.lo, 4, other)):
+            q.wait_ge(sem, n)
+            for j in js:
+                for hh in range(2):
+                    a = 64 * hh + 32 * s
+                    q.dma_start(home(j, s, hh), T["ld%d" % j][a:a + 32, :]).then_inc(S.sO, 16)
+    tot_o = 16 * 2 * 2 * 7
+
+    def chip_there(q):
+        q.wait_ge(S.bp, 8)
+        q.wait_ge(S.bq, 8)
 
     if mid:
         sy.wait_ge(S.vs, nq)
-        sy.wait_ge(S.bp, 16)
+        chip_there(sy)
         sy.wait_ge(S.bo, 32)
         sy.dma_start(T.win[:, 0:1024].bitcast(dt.uint8), T.hb[:].bitcast(dt.uint8)).then_inc(S.cw, 16)
         sy.dma_start(T.wins[:, 0:1024], T.hbs[:]).then_inc(S.cw, 16)
 
     if mid:
         W = T.wk
-        v.wait_ge(S.own, 64)
-        v.wait_ge(S.sP, 32)
+        v.wait_ge(S.kp, ncrit)
+        vw()
         sgn = 256.0 if h else -256.0
         w0 = 0 if h else 512
         jobs = []
@@ -184,37 +224,29 @@ def rank_program(g, core, T, topo):
             g.wait_ge(S.vs, n)
             return G(g.partition_broadcast(T.bj[0:128, 8 * i:8 * i + 8], T.tr[0:1, 32 * i:32 * i + 8], 128))
 
+        pa, pb = (T.cp[0:8, :], T.cr[0:8, 0:1]) if r % 2 else (T.cr[0:8, 0:1], T.cp[0:8, :])
         if bound:
-            a = 5 * (r // 2)
-            V(v.tensor_tensor(W[0:8, 0:1], T.se0[0:8, 0, a:a + 1], T.so0[0:8, 0, a:a + 1], Op.subtract))
-            V(v.tensor_tensor(W[0:8, 1:2], T.se1[0:8, 0, a:a + 1], T.so1[0:8, 0, a:a + 1], Op.subtract))
-            vw()
-            V(v.tensor_scalar(W[0:8, 2:3], W[0:8, 1:2], W[0:8, 0:1], sgn, Op.is_gt, Op.mult))
+            V(v.tensor_scalar(W[0:8, 2:3], pa, pb, sgn, Op.is_gt, Op.mult))
             vw()
             V(v.tensor_scalar(T.tt[0:8, 0:1], W[0:8, 2:3], T.li[0:8, 6:7], None, Op.add))
-            to = [4, 5, 6] if h == 0 else [3, 2, 1]
+            to = [[4, 5], [6]] if h == 0 else [[3, 2], [1]]
             jobs.append((0, row(0), "sr", w0, w0 + 512, to, 1024, "x1"))
         else:
-            v.wait_ge(S.sH, 64)
-            n = 2 * h
-            a, near = 5 * n, 1 - h
-            V(v.tensor_tensor(W[0:8, 0:2], T.se0[0:8, 0, a:a + 6:5], T.so0[0:8, 0, a:a + 6:5], Op.subtract))
-            V(v.tensor_tensor(W[0:8, 2:4], T.se1[0:8, 0, a:a + 6:5], T.so1[0:8, 0, a:a + 6:5], Op.subtract))
-            b = 4 * n + n
-            V(v.tensor_tensor(W[0:8, 8:10], T.so0[0:8, 1, b:b + 2], T.se0[0:8, 1, b + 4:b + 6], Op.subtract))
-            V(v.tensor_tensor(W[0:8, 10:12], T.so1[0:8, 1, b:b + 2], T.se1[0:8, 1, b + 4:b + 6], Op.subtract))
-            vw()
-            V(v.tensor_tensor(W[0:8, 4:6], W[0:8, 2:4], W[0:8, 0:2], Op.is_gt))
-            V(v.tensor_tensor(W[0:8, 12:13], W[0:8, 8:9], W[0:8, 10:11], Op.subtract))
-            V(v.tensor_tensor(W[0:8, 13:14], W[0:8, 11:12], W[0:8, 9:10], Op.subtract))
-            vw()
-            V(v.tensor_scalar(T.tt[0:8, 0:1], W[0:8, 4 + near:5 + near], sgn, T.li[0:8, 6:7], Op.mult, Op.add))
-            k0 = row(0)
-            V(v.tensor_scalar(W[0:8, 14:15], W[0:8, 12:13], W[0:8, 4:5], W[0:8, 10:11], Op.mult, Op.add))
-            V(v.tensor_scalar(W[0:8, 15:16], W[0:8, 13:14], W[0:8, 5:6], W[0:8, 9:10], Op.mult, Op.add))
-            V(v.tensor_tensor(W[0:8, 16:17], W[0:8, 4:5], W[0:8, 5:6], Op.add))
             i = 4 if h else 5
+            V(v.tensor_tensor(W[0:8, i:i + 1], pa, pb, Op.is_gt))
+            vw()
+            V(v.tensor_scalar(T.tt[0:8, 0:1], W[0:8, i:i + 1], sgn, T.li[0:8, 6:7], Op.mult, Op.add))
+            k0 = row(0)
             V(v.tensor_scalar(W[0:8, 18:19], W[0:8, i:i + 1], -sgn, T.li[0:8, 7:8], Op.mult, Op.add))
+            v.wait_ge(S.kf, 2 * ncrit)
+            fa, fb = (T.cx[0:8, 0:1], T.ck[0:8, :]) if h else (T.ck[0:8, :], T.cx[0:8, 0:1])
+            V(v.tensor_tensor(W[0:8, 9 - i:10 - i], fa, fb, Op.is_gt))
+            fa, fb = (T.cr[0:8, 1:4], T.cx[0:8, 1:4]) if h else (T.cx[0:8, 1:4], T.cr[0:8, 1:4])
+            V(v.tensor_tensor(W[0:8, 8:11], fa, fb, Op.subtract))
+            vw()
+            V(v.tensor_tensor(W[0:8, 14:15], W[0:8, 8:9], W[0:8, 4:5], Op.mult))
+            V(v.tensor_scalar(W[0:8, 15:16], W[0:8, 10:11], W[0:8, 5:6], W[0:8, 9:10], Op.mult, Op.add))
+            V(v.tensor_tensor(W[0:8, 16:17], W[0:8, 4:5], W[0:8, 5:6], Op.add))
             vw()
             V(v.tensor_scalar(W[0:8, 17:18], W[0:8, 16:17], sgn, sgn, Op.mult, Op.add))
             vw()
@@ -222,47 +254,52 @@ def rank_program(g, core, T, topo):
             vw()
             V(v.tensor_scalar(T.tt[0:8, 32:33], W[0:8, 19:20], W[0:8, 18:19], None, Op.add))
             k1 = row(1)
-            jobs.append((0, k0, "sr", w0, w0 + 512, [7] if h == 0 else [0], 1024, "x1"))
-            jobs.append((1, k1, "su", 0, 1024, [4, 5] if h == 0 else [3, 2], 1280, "x2"))
-        for i, k, b, wa, wb, to, col, sem in jobs:
+            jobs.append((1, k1, "su", 0, 1024, [[4, 5]] if h == 0 else [[3, 2]], 1280, "x2"))
+            jobs.append((0, k0, "sr", w0, w0 + 512, [[7]] if h == 0 else [[0]], 1024, "x1"))
+        for i, k, b, wa, wb, tos, col, sem in jobs:
             v.wait_ge(S.gs, k)
             o = 16 * i
             V(v.tensor_scalar(T.jl[:, o:o + 16:2], T.bj[:, 8 * i:8 * i + 8], T.pp[:, 0:1], None, Op.add))
             nl = V(v.tensor_scalar(T.jl[:, o + 1:o + 16:2], T.bj[:, 8 * i:8 * i + 8], T.pp[:, 1:2], None, Op.add))
             vw()
             for q in (v, sc):
-                q.wait_ge(S.bp, 16)
+                chip_there(q)
                 if i == 1:
                     q.wait_ge(S.bo, 32)
             n1 = V(v.tensor_copy(T[b][:].bitcast(dt.uint32), T.hb[:, wa:wb].bitcast(dt.uint32).indirect(T.jl[:, o:o + 16])))
             sc.wait_ge(S.vs, nl)
             n2 = A(sc.activation(T[b + "s"][:], T.hbs[:, wa:wb].indirect(T.jl[:, o:o + 16]), Act.Copy))
-            for plane in (False, True):
-                if plane:
-                    g.wait_ge(S.ss, n2)
-                    src, ds = T[b + "s"][:], [T.wins[:, col:col + 256] for k2 in to]
-                else:
-                    g.wait_ge(S.vs, n1)
-                    src, ds = T[b][:].bitcast(dt.uint8), [T.win[:, col:col + 256].bitcast(dt.uint8) for k2 in to]
-                g.remote_dma_fused([RemoteDMATransfer(dst_ids=[dst(k2) for k2 in to], dma_engine_mask=bits(off),
-                                                      remote_sem=S[sem], srcs=[src], dsts=ds)], local_sem=S.ls)
-                cl[0] += len(off)
+            for to in tos:
+                for plane in (False, True):
+                    if plane:
+                        g.wait_ge(S.ss, n2)
+                        src, ds = T[b + "s"][:], [T.wins[:, col:col + 256] for k2 in to]
+                    else:
+                        g.wait_ge(S.vs, n1)
+                        src, ds = T[b][:].bitcast(dt.uint8), [T.win[:, col:col + 256].bitcast(dt.uint8) for k2 in to]
+                    g.remote_dma_fused([RemoteDMATransfer(dst_ids=[dst(T.cores[k2]) for k2 in to],
+                                                          dma_engine_mask=bits(off), remote_sem=S[sem],
+                                                          srcs=[src], dsts=ds)], local_sem=S.ls)
+                    cl[0] += len(off)
 
-    v.wait_ge(S.own, 64)
-    v.wait_ge(S.sP, 32)
-    v.wait_ge(S.sH, 64)
+    v.wait_ge(S.xld, 16)
+    V(v.quantize_mx(T.xq[:, 0:512], T.xs[:, 0:512], T.xt[:, 0:2048]))
+    nx = V(v.quantize_mx(T.xq[:, 512:640], T.xs[:, 512:640], T.xt[:, 2048:2560]))
+
+    v.wait_ge(S.ow2, 32)
     v.wait_ge(S.sO, tot_o)
     st = (T.sta, T.stb)
     for s in range(2):
         se, so = T["se%d" % s], T["so%d" % s]
-        V(v.tensor_tensor(T.e0[0:8, 16 * s:16 * s + 16], se[0:8, 0, :], so[0:8, 0, :], Op.subtract))
         V(v.tensor_copy(st[s][0:8, 2 * h:2 * h + 2], T.li[0:8, 2 * s:2 * s + 2]))
-        for t in (1, 2, 3, 4):
-            c, i = COL[t], TI[t]
+        for t in range(5):
+            hh, f = TI[t]
             if t % 2 == 0:
-                V(v.tensor_tensor(st[s][0:8, c:c + 16], se[0:8, i, :], so[0:8, i, :], Op.subtract))
+                to = st[s][0:8, COL[t]:COL[t] + 16] if t else T.e0[0:8, 16 * s:16 * s + 16]
+                V(v.tensor_tensor(to, se[0:8, hh, :, f:f + 4], so[0:8, hh, :, f:f + 4], Op.subtract))
             else:
-                V(v.tensor_tensor(st[s][0:8, c:c + 12], so[0:8, i, 0:12], se[0:8, i, 4:16], Op.subtract))
+                V(v.tensor_tensor(st[s][0:8, COL[t]:COL[t] + 12], so[0:8, hh, 0:3, f:f + 4], se[0:8, hh, 1:4, f:f + 4],
+                                  Op.subtract))
     level = [0] * 8
     need = []
     rows = []
@@ -277,13 +314,13 @@ def rank_program(g, core, T, topo):
             else:
                 c = COL[t]
                 ea, eb = T.sta[0:8, c:c + 16:5], T.stb[0:8, c:c + 16:5]
-            cc, V0 = T.ce, 4
+            cc, np = T.ce, 4
         else:
             a, b = T.stb[0:8, 0:n], T.sta[0:8, 1:n + 1]
             c = COL[t]
             ea, eb = T.stb[0:8, c:c + 11:5], T.sta[0:8, c + 1:c + 12:5]
-            cc, V0 = T.co, 3
-        V(v.tensor_tensor(cc[0:8, 0:V0], eb, ea, Op.is_gt))
+            cc, np = T.co, 3
+        V(v.tensor_tensor(cc[0:8, 0:np], eb, ea, Op.is_gt))
         V(v.tensor_tensor(T.dd[0:8, 0:n], b, a, Op.subtract))
         vw()
         V(v.tensor_tensor(T.cd[:, 0:n], cc[:, 0:8].indirect(T.of[:, 0:n // 16]), T.dd[:, 0:n], Op.mult))
@@ -304,14 +341,13 @@ def rank_program(g, core, T, topo):
         rows.append(G(g.partition_broadcast(T.bf[0:128, 8 * t:8 * t + 8], T.tf[0:1, 32 * t:32 * t + 8], 128)))
 
     copied = {}
-    fetched = {}
 
     def ready(q, lv):
         if mid:
             q.wait_ge(S.cw, 32)
         else:
             q.wait_ge(S.vs, nq + 1)
-            q.wait_ge(S.bp, 16)
+            chip_there(q)
             q.wait_ge(S.bo, 32)
         if lv >= 1:
             q.wait_ge(S.x1, 16)
@@ -344,7 +380,7 @@ def rank_program(g, core, T, topo):
             cst[0] += 32
 
     for t in range(5):
-        lv = max(need[t], 0)
+        lv = need[t]
         w = 1024 + 256 * lv
         o = 256 * t
         fs = T.lu[:, 16 * t:16 * t + 16]
@@ -368,11 +404,9 @@ def rank_program(g, core, T, topo):
             out(t - 1)
     out(4)
 
+    v.wait_ge(S.x1, 16)
     if mid:
-        v.wait_ge(S.x1, 16)
         v.wait_ge(S.x2, 16)
-    else:
-        v.wait_ge(S.x1, 16)
     vw()
     sc.wait_ge(S.ss, cs[0])
     te.wait_ge(S.ps, 10)

@@ -8,42 +8,46 @@ SCRATCH = {
     "xt": ("sbuf", [128, 2560], "bfloat16"),
     "xq": ("sbuf", [128, 640], C8), "xs": ("sbuf", [128, 640], "uint8"),
     "hb": ("sbuf", [128, 1024], C8), "hbs": ("sbuf", [128, 1024], "uint8"),
-    "fw": ("sbuf", [128, 256], C8), "fws": ("sbuf", [128, 256], "uint8"),
     "win": ("sbuf", [128, 1536], C8), "wins": ("sbuf", [128, 1536], "uint8"),
-    "sr": ("sbuf", [128, 256], C8), "srs": ("sbuf", [128, 256], "uint8"),
-    "su": ("sbuf", [128, 256], C8), "sus": ("sbuf", [128, 256], "uint8"),
+    "pa": ("sbuf", [128, 512], C8), "pas": ("sbuf", [128, 512], "uint8"),
     "pk": ("sbuf", [128, 1280], C8), "pks": ("sbuf", [128, 1280], "uint8"),
-    "se0": ("sbuf", [128, 2, 4, 12], "int32"), "se1": ("sbuf", [128, 2, 4, 12], "int32"),
-    "so0": ("sbuf", [128, 2, 4, 12], "int32"), "so1": ("sbuf", [128, 2, 4, 12], "int32"),
+    "se": ("sbuf", [128, 2, 2, 4, 12], "int32"), "so": ("sbuf", [128, 2, 2, 4, 12], "int32"),
     "cr": ("sbuf", [128, 4], "float32"),
     "cp": ("sbuf", [128, 1], "float32"), "ck": ("sbuf", [128, 1], "float32"), "cx": ("sbuf", [128, 4], "float32"),
-    "sta": ("sbuf", [128, 68], "float32"), "stb": ("sbuf", [128, 68], "float32"),
-    "e0": ("sbuf", [128, 32], "float32"),
+    "sab": ("sbuf", [128, 2, 68], "float32"),
+    "e0": ("sbuf", [128, 2, 16], "float32"),
     "dd": ("sbuf", [128, 64], "float32"), "cd": ("sbuf", [128, 64], "float32"),
     "ce": ("sbuf", [128, 8], "float32"), "co": ("sbuf", [128, 8], "float32"),
     "wk": ("sbuf", [128, 32], "float32"),
-    "li": ("sbuf", [128, 8], "float32"), "pp": ("sbuf", [128, 2], "float32"),
+    "li": ("sbuf", [128, 8], "float32"), "pp": ("sbuf", [128, 4], "float32"),
     "pi": ("sbuf", [128, 4], "int32"), "pj": ("sbuf", [128, 4], "int32"), "p3": ("sbuf", [128, 4], "int32"),
     "of": ("sbuf", [128, 4], "uint16"),
-    "tt": ("sbuf", [128, 64], "float32"), "tr": ("sbuf", [128, 64], "float32"),
-    "bj": ("sbuf", [128, 16], "float32"), "jl": ("sbuf", [128, 32], "uint16"),
-    "tf": ("sbuf", [128, 160], "float32"), "bf": ("sbuf", [128, 40], "float32"), "lu": ("sbuf", [128, 80], "uint16"),
+    "tt": ("sbuf", [128, 32], "float32"), "tr": ("sbuf", [128, 32], "float32"),
+    "bj": ("sbuf", [128, 8], "float32"), "jl": ("sbuf", [128, 16], "uint16"),
+    "tf": ("sbuf", [128, 64], "float32"), "bf": ("sbuf", [128, 40], "float32"), "lu": ("sbuf", [128, 80], "uint16"),
     "ys": ("sbuf", [128, 1280], "float32"),
     "acc": ("psum", [128, 4096], "float32"),
 }
 for _j in range(8):
     SCRATCH["ld%d" % _j] = ("dram", [128, 3], "int32")
-SEMAPHORES = ["sD", "wld", "xld", "own", "ow2", "lp", "lh", "lo", "kp", "kf", "sO", "bp", "bq", "bo", "x1", "x2", "cw",
-              "vs", "gs", "ss", "ps", "st", "ls"]
+SEMAPHORES = ["sD", "wld", "xld", "own", "ow2", "lp", "lh", "lo", "kp", "kf", "sO", "sP", "bp", "bq", "bo", "br", "x1", "x2",
+              "cw", "vs", "gs", "ss", "ps", "st", "ls"]
 
 TI = [(0, 0), (0, 4), (0, 8), (1, 4), (1, 8)]
 COL = {1: 48, 2: 32, 3: 20, 4: 4}
 SIZE = [64, 48, 32, 32, 16]
-MID = (2, 3, 4, 5)
+OUTER, THIRD, INNER, BOUND = (0, 7), (1, 6), (2, 5), (3, 4)
+
+
+def block(r):
+    return 256 * min(r, 7 - r)
 
 
 def rank_program(g, core, T, topo):
     S = T.sem
+    r = T.rank_of(core)
+    if r is None:
+        return
 
     def dst(c):
         a = topo.addr(c)
@@ -52,38 +56,10 @@ def rank_program(g, core, T, topo):
     def bits(es):
         return sum(1 << e for e in es)
 
-    def away(r):
-        h = r // 4
-        return [k for k in ((2, 3, 0, 1) if h == 0 else (5, 4, 7, 6)) if k // 2 != r // 2]
-
-    def helper(r):
-        c = T.cores[r]
-        return [k for k in topo.cores_of(c) if T.rank_of(k) is None and topo.die(k) != topo.die(c)
-                and topo.may_write(k, T.cores[away(r)[1]])][r % 2]
-
-    def half_buf(r, k, plane):
-        c0 = 256 * (r % 4)
-        b = T[("hb" if k in MID else "win") + ("s" if plane else "")]
-        return b[:, c0:c0 + 256] if plane else b[:, c0:c0 + 256].bitcast(dt.uint8)
-
-    r = T.rank_of(core)
-    if r is None:
-        for k in range(8):
-            if helper(k) == core:
-                to = away(k)[1]
-                es = topo.engines(core, T.cores[to])
-                a = topo.addr(T.cores[to])
-                for sem, plane in ((S.bp, False), (S.bq, True)):
-                    g.wait_ge(sem, 8)
-                    g.remote_dma(half_buf(k, to, plane), T.fws[:] if plane else T.fw[:].bitcast(dt.uint8),
-                                 S.bo, S.ls, a[1], a[0], bits(es))
-                g.wait_ge(S.ls, 2 * len(es))
-        return
     v, sc, sy, te = g.vector, g.scalar, g.sync, g.tensor
     h = r // 4
-    mid = r in MID
-    bound = r == 3 + h
-    lo = r - 4 * h
+    bound, inner, third = r in BOUND, r in INNER, r in THIRD
+    mid = bound or inner
     cv, cg, cs, cl, cst = [0], [0], [0], [0], [0]
 
     def V(i):
@@ -104,15 +80,21 @@ def rank_program(g, core, T, topo):
         cs[0] += 1
         return cs[0]
 
+    def cols(k, c, n, plane):
+        b = T[("hb" if k in INNER or (k in BOUND and c >= 512) else "win") + ("s" if plane else "")]
+        return b[:, c:c + n] if plane else b[:, c:c + n].bitcast(dt.uint8)
+
     partner = r ^ 1
-    inner, outer, third = (2, 0, 1) if h == 0 else (5, 7, 6)
-    far = away(r)
+    far = [(2, 3), (0, 1), (7, 6), (5, 4)][r // 2]
+    land = [j for j in far if j in INNER + THIRD][0]
     other = [k for k in range(8) if k // 4 != h]
-    off = topo.engines(core, T.cores[far[0]])
-    on = [e for e in topo.engines(core, T.cores[partner]) if e not in off]
+    near = topo.engines(core, T.cores[partner])
+    off = topo.engines(core, T.cores[land])
+    on = [e for e in near if e not in off]
+    non, noff = len(on), len(off)
 
     def home(j, s, hh):
-        return T["so%d" % s if j % 2 else "se%d" % s][0:8, hh, j // 2, :]
+        return T["so" if j % 2 else "se"][0:8, s, hh, j // 2, :]
 
     sy.dma_start(T.d3[0:64, :], T.dm[:, 0:12]).then_inc(S.sD, 16)
     sc.dma_start(T.d3[64:128, :], T.dm[:, 8:20]).then_inc(S.sD, 16)
@@ -125,13 +107,14 @@ def rank_program(g, core, T, topo):
 
     G(g.iota(T.pi[:], [[0, 4]], 0, 1))
     fl = dict(allow_small_or_imprecise_dtypes=True)
-    G(g.iota(T.li[:, 0:2], [[512, 2]], 0, 32, **fl))
-    G(g.iota(T.li[:, 2:4], [[512, 2]], 256, 32, **fl))
+    for s in range(2):
+        b = block(4 * h + s)
+        G(g.iota(T.li[:, 2 * s:2 * s + 2], [[block(4 * h + s + 2) - b, 2]], b, 32, **fl))
     G(g.iota(T.li[:, 4:6], [[256, 2]], 1024, 32, **fl))
-    G(g.iota(T.li[:, 6:7], [[1, 1]], 0 if h else 256, 32, **fl))
-    G(g.iota(T.li[:, 7:8], [[1, 1]], 256 if h else 512, 32, **fl))
+    if mid:
+        G(g.iota(T.li[:, 6:7], [[1, 1]], 512 if inner else 256, 32, **fl))
     nconst = cg[0]
-    for b in ("cr", "sta", "stb", "dd", "ce", "co", "tt"):
+    for b in ("cr", "sab", "dd", "ce", "co") + (("tt",) if mid else ()):
         V(v.memset(T[b][:], 0.0))
     v.wait_ge(S.gs, nconst)
     V(v.tensor_scalar(T.pj[:], T.pi[:], 15, None, Op.bitwise_and))
@@ -139,6 +122,9 @@ def rank_program(g, core, T, topo):
     vw()
     V(v.tensor_copy(T.pp[:, 0:1], T.pj[:, 0:1]))
     V(v.tensor_scalar(T.pp[:, 1:2], T.pj[:, 0:1], 16.0, None, Op.add))
+    if bound:
+        V(v.tensor_scalar(T.pp[:, 2:3], T.pj[:, 0:1], -512.0, None, Op.add))
+        V(v.tensor_scalar(T.pp[:, 3:4], T.pj[:, 0:1], -496.0, None, Op.add))
     V(v.tensor_copy(T.of[:], T.p3[:]))
 
     g.wait_ge(S.sD, 32)
@@ -153,172 +139,195 @@ def rank_program(g, core, T, topo):
     cl[0] += 3
 
     m, n2 = r // 2, 2 * h
-    o0, o1 = (T.so0, T.so1) if r % 2 else (T.se0, T.se1)
+    o = T.so if r % 2 else T.se
     v.wait_ge(S.own, 32)
     vw()
-    V(v.tensor_tensor(T.cr[0:8, 0:1], o1[0:8, 0, m, m:m + 1], o0[0:8, 0, m, m:m + 1], Op.subtract))
-    c = 4 + n2
-    if r in (inner, third):
-        V(v.tensor_tensor(T.cr[0:8, 1:2], o0[0:8, 0, m, c:c + 1], o1[0:8, 0, m, c:c + 1], Op.subtract))
-        V(v.tensor_tensor(T.cr[0:8, 2:3], o0[0:8, 0, m, c + 1:c + 2], o1[0:8, 0, m, c:c + 1], Op.subtract))
-        V(v.tensor_tensor(T.cr[0:8, 3:4], o1[0:8, 0, m, c + 1:c + 2], o0[0:8, 0, m, c + 1:c + 2], Op.subtract))
+    V(v.tensor_tensor(T.cr[0:8, 0:1], o[0:8, 1, 0, m, m:m + 1], o[0:8, 0, 0, m, m:m + 1], Op.subtract))
+    if inner or third:
+        c = 4 + n2
+        V(v.tensor_tensor(T.cr[0:8, 1:2], o[0:8, 0, 0, m, c:c + 1], o[0:8, 1, 0, m, c:c + 1], Op.subtract))
+        V(v.tensor_tensor(T.cr[0:8, 2:3], o[0:8, 0, 0, m, c + 1:c + 2], o[0:8, 1, 0, m, c:c + 1], Op.subtract))
+        V(v.tensor_tensor(T.cr[0:8, 3:4], o[0:8, 1, 0, m, c + 1:c + 2], o[0:8, 0, 0, m, c + 1:c + 2], Op.subtract))
     g.wait_ge(S.vs, cv[0])
     if mid:
-        to, es, sem, src, land = partner, on, S.kp, T.cr[:, 0:1], T.cp[:]
-    elif r == outer:
-        to, es, sem, src, land = inner, off, S.kf, T.cr[:, 0:1], T.ck[:]
+        to, es, sem, src, place = partner, on, S.kp, T.cr[:, 0:1], T.cp[:]
+    elif third:
+        to, es, sem, src, place = land, off, S.kf, T.cr[:], T.cx[:]
     else:
-        to, es, sem, src, land = inner, off, S.kf, T.cr[:], T.cx[:]
+        to, es, sem, src, place = land, off, S.kf, T.cr[:, 0:1], T.ck[:]
     a = topo.addr(T.cores[to])
-    g.remote_dma(land, src, sem, S.ls, a[1], a[0], bits(es))
-    ncrit = len(es)
-    cl[0] += ncrit
+    g.remote_dma(place, src, sem, S.ls, a[1], a[0], bits(es))
+    cl[0] += len(es)
 
-    c0 = 256 * lo
+    c0 = block(r)
     v.wait_ge(S.wld, 16)
     nq = V(v.quantize_mx(T.hb[:, c0:c0 + 256], T.hbs[:, c0:c0 + 256], T.wt[:]))
-    if not mid:
-        V(v.quantize_mx(T.win[:, c0:c0 + 256], T.wins[:, c0:c0 + 256], T.wt[:]))
+    V(v.quantize_mx(T.win[:, c0:c0 + 256], T.wins[:, c0:c0 + 256], T.wt[:]))
     g.wait_ge(S.vs, nq)
     for plane in (False, True):
         src = T.hbs[:, c0:c0 + 256] if plane else T.hb[:, c0:c0 + 256].bitcast(dt.uint8)
         g.remote_dma_fused([
-            RemoteDMATransfer(dst_ids=[dst(T.cores[partner]), dst(helper(r))], dma_engine_mask=bits(on),
-                              remote_sem=S.bq if plane else S.bp, srcs=[src],
-                              dsts=[half_buf(r, partner, plane), T.fws[:] if plane else T.fw[:].bitcast(dt.uint8)]),
-            RemoteDMATransfer(dst_ids=[dst(T.cores[far[0]])], dma_engine_mask=bits(off), remote_sem=S.bo,
-                              srcs=[src], dsts=[half_buf(r, far[0], plane)])], local_sem=S.ls)
-        cl[0] += len(on) + len(off)
+            RemoteDMATransfer(dst_ids=[dst(T.cores[partner])], dma_engine_mask=bits(on), remote_sem=S.bq if plane else S.bp,
+                              srcs=[src], dsts=[cols(partner, c0, 256, plane)]),
+            RemoteDMATransfer(dst_ids=[dst(T.cores[land])], dma_engine_mask=bits(off), remote_sem=S.bo,
+                              srcs=[src], dsts=[cols(land, c0, 256, plane)])], local_sem=S.ls)
+        cl[0] += non + noff
+    v.wait_ge(S.xld, 16)
+    V(v.quantize_mx(T.xq[:, 0:512], T.xs[:, 0:512], T.xt[:, 0:2048]))
+    nx = V(v.quantize_mx(T.xq[:, 512:640], T.xs[:, 512:640], T.xt[:, 2048:2560]))
 
-    for s, q in ((0, sy), (1, sc)):
-        for sem, n, js in ((S.lp, 1, [partner]), (S.lh, 2, far), (S.lo, 4, other)):
-            q.wait_ge(sem, n)
-            for j in js:
-                for hh in range(2):
+    for hh in range(2):
+        for s, q in ((0, sy), (1, sc)):
+            for sem, n, js in ((S.lp, 1, [partner]), (S.lh, 2, far), (S.lo, 4, other)):
+                q.wait_ge(sem, n)
+                for j in js:
                     a = 64 * hh + 32 * s
-                    q.dma_start(home(j, s, hh), T["ld%d" % j][a:a + 32, :]).then_inc(S.sO, 16)
-    tot_o = 16 * 2 * 2 * 7
+                    q.dma_start(home(j, s, hh), T["ld%d" % j][a:a + 32, :]).then_inc(S.sP if hh else S.sO, 16)
+    nl = 16 * 2 * 7
 
     def chip_there(q):
-        q.wait_ge(S.bp, 8)
-        q.wait_ge(S.bq, 8)
+        q.wait_ge(S.bp, non)
+        q.wait_ge(S.bq, non)
+
+    def half_there(q):
+        chip_there(q)
+        if inner or third:
+            q.wait_ge(S.bo, 4 * noff)
+        else:
+            q.wait_ge(S.br, 2 * (non if mid else len(near)))
+
+    def relay(src, c, w, sem, plane, es):
+        a = topo.addr(T.cores[partner])
+        to = T.wins[:, c:c + w] if plane else T.win[:, c:c + w].bitcast(dt.uint8)
+        g.remote_dma(to, src if src else to, sem, S.ls, a[1], a[0], bits(es))
+        cl[0] += len(es)
+
+    def to_win(a, n):
+        sy.dma_start(T.win[:, a:a + n].bitcast(dt.uint8), T.hb[:, a:a + n].bitcast(dt.uint8)).then_inc(S.cw, 16)
+        sy.dma_start(T.wins[:, a:a + n], T.hbs[:, a:a + n]).then_inc(S.cw, 16)
 
     if mid:
-        sy.wait_ge(S.vs, nq)
         chip_there(sy)
-        sy.wait_ge(S.bo, 32)
-        sy.dma_start(T.win[:, 0:1024].bitcast(dt.uint8), T.hb[:].bitcast(dt.uint8)).then_inc(S.cw, 16)
-        sy.dma_start(T.wins[:, 0:1024], T.hbs[:]).then_inc(S.cw, 16)
+        to_win(block(partner), 256)
+        if inner:
+            half_there(sy)
+            to_win(0, 512)
+    ncw = 64 if inner else 32
+
+    def send(k, x, sem, c, n1, n2):
+        a = topo.addr(T.cores[k])
+        g.wait_ge(S.vs, n1)
+        g.remote_dma(T.win[:, c:c + 256].bitcast(dt.uint8), T.pa[:, x:x + 256].bitcast(dt.uint8), sem, S.ls, a[1], a[0], bits(off))
+        g.wait_ge(S.ss, n2)
+        g.remote_dma(T.wins[:, c:c + 256], T.pas[:, x:x + 256], sem, S.ls, a[1], a[0], bits(off))
+        cl[0] += 2 * noff
+
+    def pick(x, wa, wb, fs, nlist, buf, src):
+        n1 = V(v.tensor_copy(T[buf][:, x:x + 256].bitcast(dt.uint32), T[src][:, wa:wb].bitcast(dt.uint32).indirect(fs)))
+        sc.wait_ge(S.vs, nlist)
+        return n1, A(sc.activation(T[buf + "s"][:, x:x + 256], T[src + "s"][:, wa:wb].indirect(fs), Act.Copy))
+
+    stat = {}
 
     if mid:
         W = T.wk
-        v.wait_ge(S.kp, ncrit)
+        v.wait_ge(S.kp, non)
         vw()
-        sgn = 256.0 if h else -256.0
-        w0 = 0 if h else 512
-        jobs = []
-
-        def row(i):
-            vw()
-            n = V(v.transpose(T.tr[0:32, 32 * i:32 * i + 32], T.tt[0:32, 32 * i:32 * i + 32]))
-            g.wait_ge(S.vs, n)
-            return G(g.partition_broadcast(T.bj[0:128, 8 * i:8 * i + 8], T.tr[0:1, 32 * i:32 * i + 8], 128))
-
         pa, pb = (T.cp[0:8, :], T.cr[0:8, 0:1]) if r % 2 else (T.cr[0:8, 0:1], T.cp[0:8, :])
         if bound:
-            V(v.tensor_scalar(W[0:8, 2:3], pa, pb, sgn, Op.is_gt, Op.mult))
+            V(v.tensor_scalar(W[0:8, 2:3], pa, pb, -256.0, Op.is_gt, Op.mult))
             vw()
             V(v.tensor_scalar(T.tt[0:8, 0:1], W[0:8, 2:3], T.li[0:8, 6:7], None, Op.add))
-            to = [[4, 5], [6]] if h == 0 else [[3, 2], [1]]
-            jobs.append((0, row(0), "sr", w0, w0 + 512, to, 1024, "x1"))
         else:
             i = 4 if h else 5
             V(v.tensor_tensor(W[0:8, i:i + 1], pa, pb, Op.is_gt))
-            vw()
-            V(v.tensor_scalar(T.tt[0:8, 0:1], W[0:8, i:i + 1], sgn, T.li[0:8, 6:7], Op.mult, Op.add))
-            k0 = row(0)
-            V(v.tensor_scalar(W[0:8, 18:19], W[0:8, i:i + 1], -sgn, T.li[0:8, 7:8], Op.mult, Op.add))
-            v.wait_ge(S.kf, 2 * ncrit)
+            v.wait_ge(S.kf, 2 * noff)
             fa, fb = (T.cx[0:8, 0:1], T.ck[0:8, :]) if h else (T.ck[0:8, :], T.cx[0:8, 0:1])
             V(v.tensor_tensor(W[0:8, 9 - i:10 - i], fa, fb, Op.is_gt))
             fa, fb = (T.cr[0:8, 1:4], T.cx[0:8, 1:4]) if h else (T.cx[0:8, 1:4], T.cr[0:8, 1:4])
             V(v.tensor_tensor(W[0:8, 8:11], fa, fb, Op.subtract))
             vw()
+            V(v.tensor_scalar(W[0:8, 18:19], W[0:8, i:i + 1], 256.0, T.li[0:8, 6:7], Op.mult, Op.add))
             V(v.tensor_tensor(W[0:8, 14:15], W[0:8, 8:9], W[0:8, 4:5], Op.mult))
             V(v.tensor_scalar(W[0:8, 15:16], W[0:8, 10:11], W[0:8, 5:6], W[0:8, 9:10], Op.mult, Op.add))
             V(v.tensor_tensor(W[0:8, 16:17], W[0:8, 4:5], W[0:8, 5:6], Op.add))
             vw()
-            V(v.tensor_scalar(W[0:8, 17:18], W[0:8, 16:17], sgn, sgn, Op.mult, Op.add))
+            V(v.tensor_scalar(W[0:8, 17:18], W[0:8, 16:17], -256.0, -256.0, Op.mult, Op.add))
             vw()
             V(v.tensor_scalar(W[0:8, 19:20], W[0:8, 15:16], W[0:8, 14:15], W[0:8, 17:18], Op.is_gt, Op.mult))
             vw()
-            V(v.tensor_scalar(T.tt[0:8, 32:33], W[0:8, 19:20], W[0:8, 18:19], None, Op.add))
-            k1 = row(1)
-            jobs.append((1, k1, "su", 0, 1024, [[4, 5]] if h == 0 else [[3, 2]], 1280, "x2"))
-            jobs.append((0, k0, "sr", w0, w0 + 512, [[7]] if h == 0 else [[0]], 1024, "x1"))
-        for i, k, b, wa, wb, tos, col, sem in jobs:
-            v.wait_ge(S.gs, k)
-            o = 16 * i
-            V(v.tensor_scalar(T.jl[:, o:o + 16:2], T.bj[:, 8 * i:8 * i + 8], T.pp[:, 0:1], None, Op.add))
-            nl = V(v.tensor_scalar(T.jl[:, o + 1:o + 16:2], T.bj[:, 8 * i:8 * i + 8], T.pp[:, 1:2], None, Op.add))
-            vw()
-            for q in (v, sc):
-                chip_there(q)
-                if i == 1:
-                    q.wait_ge(S.bo, 32)
-            n1 = V(v.tensor_copy(T[b][:].bitcast(dt.uint32), T.hb[:, wa:wb].bitcast(dt.uint32).indirect(T.jl[:, o:o + 16])))
-            sc.wait_ge(S.vs, nl)
-            n2 = A(sc.activation(T[b + "s"][:], T.hbs[:, wa:wb].indirect(T.jl[:, o:o + 16]), Act.Copy))
-            for to in tos:
-                for plane in (False, True):
-                    if plane:
-                        g.wait_ge(S.ss, n2)
-                        src, ds = T[b + "s"][:], [T.wins[:, col:col + 256] for k2 in to]
-                    else:
-                        g.wait_ge(S.vs, n1)
-                        src, ds = T[b][:].bitcast(dt.uint8), [T.win[:, col:col + 256].bitcast(dt.uint8) for k2 in to]
-                    g.remote_dma_fused([RemoteDMATransfer(dst_ids=[dst(T.cores[k2]) for k2 in to],
-                                                          dma_engine_mask=bits(off), remote_sem=S[sem],
-                                                          srcs=[src], dsts=ds)], local_sem=S.ls)
-                    cl[0] += len(off)
+            V(v.tensor_scalar(T.tt[0:8, 0:1], W[0:8, 19:20], W[0:8, 18:19], None, Op.add))
+        vw()
+        n = V(v.transpose(T.tr[0:32, :], T.tt[0:32, :]))
+        g.wait_ge(S.vs, n)
+        n = G(g.partition_broadcast(T.bj[:], T.tr[0:1, 0:8], 128))
+        v.wait_ge(S.gs, n)
+        V(v.tensor_scalar(T.jl[:, 0:16:2], T.bj[:], T.pp[:, 0:1], None, Op.add))
+        n = V(v.tensor_scalar(T.jl[:, 1:16:2], T.bj[:], T.pp[:, 1:2], None, Op.add))
+        vw()
+        for q in (v, sc):
+            (chip_there if bound else half_there)(q)
+        if bound:
+            n1, n2 = pick(0, 512, 1024, T.jl[:], n, "pa", "hb")
+            stat[0] = ("pa", 0, n1, n2)
+            for k in ((4, 6) if h == 0 else (3, 1)):
+                send(k, 0, S.x1, 1024, n1, n2)
+        else:
+            n1, n2 = pick(256, 0, 1024, T.jl[:], n, "pa", "hb")
+            stat[1] = ("pa", 256, n1, n2)
+            to = (4, 5) if h == 0 else (3, 2)
+            half_there(g)
+            relay(T.hb[:, 0:512].bitcast(dt.uint8), 0, 512, S.br, False, on)
+            send(to[0], 256, S.x2, 1280, n1, n2)
+            relay(T.hbs[:, 0:512], 0, 512, S.br, True, on)
+            send(to[1], 256, S.x2, 1280, n1, n2)
 
-    v.wait_ge(S.xld, 16)
-    V(v.quantize_mx(T.xq[:, 0:512], T.xs[:, 0:512], T.xt[:, 0:2048]))
-    nx = V(v.quantize_mx(T.xq[:, 512:640], T.xs[:, 512:640], T.xt[:, 2048:2560]))
+    if third:
+        half_there(g)
+        for plane in (False, True):
+            relay(None, 512, 512, S.br, plane, near)
 
-    v.wait_ge(S.ow2, 32)
-    v.wait_ge(S.sO, tot_o)
-    st = (T.sta, T.stb)
-    for s in range(2):
-        se, so = T["se%d" % s], T["so%d" % s]
-        V(v.tensor_copy(st[s][0:8, 2 * h:2 * h + 2], T.li[0:8, 2 * s:2 * s + 2]))
-        for t in range(5):
-            hh, f = TI[t]
-            if t % 2 == 0:
-                to = st[s][0:8, COL[t]:COL[t] + 16] if t else T.e0[0:8, 16 * s:16 * s + 16]
-                V(v.tensor_tensor(to, se[0:8, hh, :, f:f + 4], so[0:8, hh, :, f:f + 4], Op.subtract))
-            else:
-                V(v.tensor_tensor(st[s][0:8, COL[t]:COL[t] + 12], so[0:8, hh, 0:3, f:f + 4], se[0:8, hh, 1:4, f:f + 4],
-                                  Op.subtract))
+    def numbers(t):
+        hh, f = TI[t]
+        if t % 2 == 0:
+            to = T.sab[0:8, :, COL[t]:COL[t] + 16] if t else T.e0[0:8, :, :]
+            V(v.tensor_tensor(to, T.se[0:8, :, hh, :, f:f + 4], T.so[0:8, :, hh, :, f:f + 4], Op.subtract))
+        else:
+            V(v.tensor_tensor(T.sab[0:8, :, COL[t]:COL[t] + 12], T.so[0:8, :, hh, 0:3, f:f + 4],
+                              T.se[0:8, :, hh, 1:4, f:f + 4], Op.subtract))
+
     level = [0] * 8
     need = []
-    rows = []
+    nlist = {}
+    for s in range(2):
+        V(v.tensor_copy(T.sab[0:8, s, 2 * h:2 * h + 2], T.li[0:8, 2 * s:2 * s + 2]))
+    v.wait_ge(S.own, 32)
+    v.wait_ge(S.sO, nl)
+    for t in range(3):
+        numbers(t)
+    v.wait_ge(S.ow2, 32)
+    v.wait_ge(S.sP, nl)
+    for t in (3, 4):
+        numbers(t)
+
+    t0 = 1 if bound else 0
+    first, groups = range(t0, 1 if inner else 2), []
     for t in range(5):
         n = SIZE[t]
         odd = t % 2
         vw()
         if not odd:
-            a, b = T.sta[0:8, 0:n], T.stb[0:8, 0:n]
+            a, b = T.sab[0:8, 0, 0:n], T.sab[0:8, 1, 0:n]
             if t == 0:
-                ea, eb = T.e0[0:8, 0:16:5], T.e0[0:8, 16:32:5]
+                ea, eb = T.e0[0:8, 0, 0:16:5], T.e0[0:8, 1, 0:16:5]
             else:
                 c = COL[t]
-                ea, eb = T.sta[0:8, c:c + 16:5], T.stb[0:8, c:c + 16:5]
+                ea, eb = T.sab[0:8, 0, c:c + 16:5], T.sab[0:8, 1, c:c + 16:5]
             cc, np = T.ce, 4
         else:
-            a, b = T.stb[0:8, 0:n], T.sta[0:8, 1:n + 1]
+            a, b = T.sab[0:8, 1, 0:n], T.sab[0:8, 0, 1:n + 1]
             c = COL[t]
-            ea, eb = T.stb[0:8, c:c + 11:5], T.sta[0:8, c + 1:c + 12:5]
+            ea, eb = T.sab[0:8, 1, c:c + 11:5], T.sab[0:8, 0, c + 1:c + 12:5]
             cc, np = T.co, 3
         V(v.tensor_tensor(cc[0:8, 0:np], eb, ea, Op.is_gt))
         V(v.tensor_tensor(T.dd[0:8, 0:n], b, a, Op.subtract))
@@ -332,33 +341,50 @@ def rank_program(g, core, T, topo):
         if t < 2:
             pos = (4 + t) if h == 0 else (3 - t)
             vw()
-            V(v.tensor_copy(st[pos % 2][0:8, pos // 2:pos // 2 + 1], T.li[0:8, 4 + t:5 + t]))
+            V(v.tensor_copy(T.sab[0:8, pos % 2, pos // 2:pos // 2 + 1], T.li[0:8, 4 + t:5 + t]))
             level[pos] = 1 + t
         need.append(level[r])
-        vw()
-        k = V(v.transpose(T.tf[0:32, 32 * t:32 * t + 32], st[r % 2][0:32, r // 2:r // 2 + 32]))
-        g.wait_ge(S.vs, k)
-        rows.append(G(g.partition_broadcast(T.bf[0:128, 8 * t:8 * t + 8], T.tf[0:1, 32 * t:32 * t + 8], 128)))
+        if t > 1 or t in first:
+            vw()
+            k = V(v.transpose(T.tf[0:32, 8 * t:8 * t + 32], T.sab[0:32, r % 2, r // 2:r // 2 + 32]))
+        if t == first[-1] or t == 4:
+            t0 = first[0] if t < 2 else 2
+            g.wait_ge(S.vs, k)
+            groups.append((t0, t + 1, G(g.partition_broadcast(T.bf[0:128, 8 * t0:8 * t + 8], T.tf[0:1, 8 * t0:8 * t + 8], 128))))
+    for t0, t1, k in groups:
+        v.wait_ge(S.gs, k)
+        fr = T.bf[:, 8 * t0:8 * t1]
+        o = 2 if bound and t1 == 2 else 0
+        V(v.tensor_scalar(T.lu[:, 16 * t0:16 * t1:2], fr, T.pp[:, o:o + 1], None, Op.add))
+        n = V(v.tensor_scalar(T.lu[:, 16 * t0 + 1:16 * t1:2], fr, T.pp[:, o + 1:o + 2], None, Op.add))
+        for t in range(t0, t1):
+            nlist[t] = n
+
+    if bound or third:
+        g.wait_ge(S.x1, 2 * noff)
+        for plane in (False, True):
+            relay(None, 1024, 256, S.x1, plane, near)
 
     copied = {}
+    nx1 = 2 * (noff if bound or third else len(near))
 
-    def ready(q, lv):
+    def ready(q, t, lv):
+        if inner and t == 0:
+            half_there(q)
+            return "pa", "hb", 0, 1024
         if mid:
-            q.wait_ge(S.cw, 32)
-        else:
-            q.wait_ge(S.vs, nq + 1)
-            chip_there(q)
-            q.wait_ge(S.bo, 32)
+            q.wait_ge(S.cw, ncw)
         if lv >= 1:
-            q.wait_ge(S.x1, 16)
+            q.wait_ge(S.x1, nx1)
         if lv >= 2:
-            q.wait_ge(S.x2, 16)
-
-    nlist = []
-    for t in range(5):
-        v.wait_ge(S.gs, rows[t])
-        V(v.tensor_scalar(T.lu[:, 16 * t:16 * t + 16:2], T.bf[:, 8 * t:8 * t + 8], T.pp[:, 0:1], None, Op.add))
-        nlist.append(V(v.tensor_scalar(T.lu[:, 16 * t + 1:16 * t + 16:2], T.bf[:, 8 * t:8 * t + 8], T.pp[:, 1:2], None, Op.add)))
+            q.wait_ge(S.x2, 2 * noff)
+        if bound and t == 1:
+            return "pk", "win", 512, 1280
+        if not mid and t < (1 if third else 2):
+            chip_there(q)
+            return "pk", "win", 0, 512
+        half_there(q)
+        return "pk", "win", 0, 1024 + 256 * lv
 
     def out(t):
         o = 256 * t
@@ -380,16 +406,13 @@ def rank_program(g, core, T, topo):
             cst[0] += 32
 
     for t in range(5):
-        lv = need[t]
-        w = 1024 + 256 * lv
-        o = 256 * t
-        fs = T.lu[:, 16 * t:16 * t + 16]
-        vw()
-        ready(v, lv)
-        n1 = V(v.tensor_copy(T.pk[:, o:o + 256].bitcast(dt.uint32), T.win[:, 0:w].bitcast(dt.uint32).indirect(fs)))
-        sc.wait_ge(S.vs, nlist[t])
-        ready(sc, lv)
-        n2 = A(sc.activation(T.pks[:, o:o + 256], T.wins[:, 0:w].indirect(fs), Act.Copy))
+        if t not in stat:
+            vw()
+            for q in (v, sc):
+                buf, src, wa, wb = ready(q, t, need[t])
+            n1, n2 = pick(256 * t, wa, wb, T.lu[:, 16 * t:16 * t + 16], nlist[t], buf, src)
+            stat[t] = (buf, 256 * t, n1, n2)
+        buf, x, n1, n2 = stat[t]
         te.wait_ge(S.vs, max(n1, nx))
         te.wait_ge(S.ss, n2)
         if t == 4:
@@ -397,16 +420,16 @@ def rank_program(g, core, T, topo):
             te.wait_ge(S.ss, copied[0][1])
         for k in range(2):
             e = 512 * ((2 * t + k) % 8)
-            c = o + 128 * k
-            te.matmul_mx(T.acc[:, e:e + 128], T.pk[:, c:c + 128], T.pks[:, c:c + 128],
+            c = x + 128 * k
+            te.matmul_mx(T.acc[:, e:e + 128], T[buf][:, c:c + 128], T[buf + "s"][:, c:c + 128],
                          T.xq[:, 128 * t:128 * t + 128], T.xs[:, 128 * t:128 * t + 128], True, True).then_inc(S.ps, 1)
         if t > 0:
             out(t - 1)
     out(4)
 
-    v.wait_ge(S.x1, 16)
+    v.wait_ge(S.x1, nx1)
     if mid:
-        v.wait_ge(S.x2, 16)
+        v.wait_ge(S.x2, 2 * noff)
     vw()
     sc.wait_ge(S.ss, cs[0])
     te.wait_ge(S.ps, 10)

@@ -9,19 +9,21 @@ SCRATCH = {
     "xq": ("sbuf", [128, 640], C8), "xs": ("sbuf", [128, 640], "uint8"),
     "hb": ("sbuf", [128, 1024], C8), "hbs": ("sbuf", [128, 1024], "uint8"),
     "win": ("sbuf", [128, 1536], C8), "wins": ("sbuf", [128, 1536], "uint8"),
-    "pa": ("sbuf", [128, 512], C8), "pas": ("sbuf", [128, 512], "uint8"),
+    "pa": ("sbuf", [128, 1024], C8), "pas": ("sbuf", [128, 1024], "uint8"),
+    "hw": ("sbuf", [128, 256], C8), "hws": ("sbuf", [128, 256], "uint8"),
     "pk": ("sbuf", [128, 1280], C8), "pks": ("sbuf", [128, 1280], "uint8"),
     "se": ("sbuf", [128, 2, 2, 4, 12], "int32"), "so": ("sbuf", [128, 2, 2, 4, 12], "int32"),
     "cr": ("sbuf", [128, 4], "float32"),
-    "cp": ("sbuf", [128, 1], "float32"), "ck": ("sbuf", [128, 1], "float32"), "cx": ("sbuf", [128, 4], "float32"),
+    "cp": ("sbuf", [128, 4], "float32"), "ck": ("sbuf", [128, 4], "float32"), "cx": ("sbuf", [128, 4], "float32"),
     "sab": ("sbuf", [128, 2, 68], "float32"),
     "e0": ("sbuf", [128, 2, 16], "float32"),
     "dd": ("sbuf", [128, 64], "float32"), "cd": ("sbuf", [128, 64], "float32"),
     "ce": ("sbuf", [128, 8], "float32"), "co": ("sbuf", [128, 8], "float32"),
     "wk": ("sbuf", [128, 32], "float32"),
-    "li": ("sbuf", [128, 8], "float32"), "pp": ("sbuf", [128, 4], "float32"),
+    "li": ("sbuf", [128, 12], "float32"), "pp": ("sbuf", [128, 4], "float32"),
     "pi": ("sbuf", [128, 4], "int32"), "pj": ("sbuf", [128, 4], "int32"), "p3": ("sbuf", [128, 4], "int32"),
-    "of": ("sbuf", [128, 4], "uint16"),
+    "ph": ("sbuf", [128, 4], "int32"), "pf": ("sbuf", [128, 2], "float32"),
+    "of": ("sbuf", [128, 4], "uint16"), "oz": ("sbuf", [128, 4], "uint16"),
     "tt": ("sbuf", [128, 32], "float32"), "tr": ("sbuf", [128, 32], "float32"),
     "bj": ("sbuf", [128, 8], "float32"), "jl": ("sbuf", [128, 16], "uint16"),
     "tf": ("sbuf", [128, 64], "float32"), "bf": ("sbuf", [128, 40], "float32"), "lu": ("sbuf", [128, 80], "uint16"),
@@ -30,24 +32,32 @@ SCRATCH = {
 }
 for _j in range(8):
     SCRATCH["ld%d" % _j] = ("dram", [128, 3], "int32")
-SEMAPHORES = ["sD", "wld", "xld", "own", "ow2", "lp", "lh", "lo", "kp", "kf", "sO", "sP", "bp", "bq", "bo", "br", "x1", "x2",
-              "cw", "vs", "gs", "ss", "ps", "st", "ls"]
+SEMAPHORES = ["sD", "wld", "xld", "own", "ow2", "lp", "lh", "lo", "kp", "kf", "sO", "sP", "bp", "bps", "bo", "bos", "br", "brs",
+              "x1", "x1s", "x2", "x2s", "rw", "rws", "hs", "hss", "cw", "vs", "gs", "ss", "ps", "st", "ls"]
 
 TI = [(0, 0), (0, 4), (0, 8), (1, 4), (1, 8)]
-COL = {1: 48, 2: 32, 3: 20, 4: 4}
-SIZE = [64, 48, 32, 32, 16]
 OUTER, THIRD, INNER, BOUND = (0, 7), (1, 6), (2, 5), (3, 4)
+OUTSIDE = {2: 6, 3: 7, 4: 0, 5: 1}
+X2_TO = {2: 4, 1: 5, 5: 3, 6: 2}
 
 
 def block(r):
     return 256 * min(r, 7 - r)
 
 
+def pairs(r, t):
+    m = r // 2
+    d = (5 - t) // 2
+    return list(range(max(0, m - d), min(2, m + d - 1) + 1)) if t % 2 else list(range(max(0, m - d), min(3, m + d) + 1))
+
+
+def ranks(r, ts):
+    return sorted({2 * k + t % 2 + i for t in ts for k in pairs(r, t) for i in range(2)})
+
+
 def rank_program(g, core, T, topo):
     S = T.sem
     r = T.rank_of(core)
-    if r is None:
-        return
 
     def dst(c):
         a = topo.addr(c)
@@ -56,10 +66,37 @@ def rank_program(g, core, T, topo):
     def bits(es):
         return sum(1 << e for e in es)
 
+    def sem(name, plane):
+        return S[name + ("s" if plane else "")]
+
+    def view(b, c, n, plane):
+        return T[b + "s"][:, c:c + n] if plane else T[b][:, c:c + n].bitcast(dt.uint8)
+
+    def helper(k):
+        c, to = T.cores[k], T.cores[OUTSIDE[k]]
+        return [x for x in topo.cores_of(c) if x not in T.cores and (topo.die(x) == topo.die(c)) == (k % 2 == 1)
+                and topo.may_write(x, to)][0]
+
+    if r is None:
+        for k in INNER + BOUND:
+            if core == helper(k):
+                to = sorted([OUTSIDE[k], OUTSIDE[k] ^ 1], key=lambda j: j in OUTER)
+                es = topo.engines(core, T.cores[to[0]])
+                n = len([e for e in topo.engines(T.cores[k], core) if e not in es])
+                for plane in (False, True):
+                    g.wait_ge(sem("hs", plane), n)
+                    g.remote_dma_fused([RemoteDMATransfer(
+                        dst_ids=[dst(T.cores[j]) for j in to], dma_engine_mask=bits(es), remote_sem=sem("rw", plane),
+                        srcs=[view("hw", 0, 256, plane)],
+                        dsts=[view("win", 1024 + 256 * (k % 2), 256, plane) for j in to])], local_sem=S.ls)
+                g.wait_ge(S.ls, 2 * len(es))
+        return
+
     v, sc, sy, te = g.vector, g.scalar, g.sync, g.tensor
     h = r // 4
-    bound, inner, third = r in BOUND, r in INNER, r in THIRD
+    bound, inner, third, outer = r in BOUND, r in INNER, r in THIRD, r in OUTER
     mid = bound or inner
+    hand = inner or third
     cv, cg, cs, cl, cst = [0], [0], [0], [0], [0]
 
     def V(i):
@@ -67,8 +104,8 @@ def rank_program(g, core, T, topo):
         cv[0] += 1
         return cv[0]
 
-    def vw():
-        v.wait_ge(S.vs, cv[0])
+    def vw(n=None):
+        v.wait_ge(S.vs, n or cv[0])
 
     def G(i):
         i.then_inc(S.gs, 1)
@@ -80,9 +117,8 @@ def rank_program(g, core, T, topo):
         cs[0] += 1
         return cs[0]
 
-    def cols(k, c, n, plane):
-        b = T[("hb" if k in INNER or (k in BOUND and c >= 512) else "win") + ("s" if plane else "")]
-        return b[:, c:c + n] if plane else b[:, c:c + n].bitcast(dt.uint8)
+    def home_of_w(k, c):
+        return "hb" if k in INNER + THIRD or (k in BOUND and c >= 512) else "win"
 
     partner = r ^ 1
     far = [(2, 3), (0, 1), (7, 6), (5, 4)][r // 2]
@@ -91,7 +127,8 @@ def rank_program(g, core, T, topo):
     near = topo.engines(core, T.cores[partner])
     off = topo.engines(core, T.cores[land])
     on = [e for e in near if e not in off]
-    non, noff = len(on), len(off)
+    non, noff, nall = len(on), len(off), len(near)
+    nx1 = noff if bound else nall
 
     def home(j, s, hh):
         return T["so" if j % 2 else "se"][0:8, s, hh, j // 2, :]
@@ -109,33 +146,29 @@ def rank_program(g, core, T, topo):
     fl = dict(allow_small_or_imprecise_dtypes=True)
     for s in range(2):
         b = block(4 * h + s)
-        G(g.iota(T.li[:, 2 * s:2 * s + 2], [[block(4 * h + s + 2) - b, 2]], b, 32, **fl))
-    G(g.iota(T.li[:, 4:6], [[256, 2]], 1024, 32, **fl))
-    if mid:
-        G(g.iota(T.li[:, 6:7], [[1, 1]], 512 if inner else 256, 32, **fl))
+        G(g.iota(T.li[:, 4 * s + 2 * h:4 * s + 2 * h + 2], [[block(4 * h + s + 2) - b, 2]], b, 32, **fl))
+        o = 4 * s + 2 * (1 - h)
+        if mid and (h == 0) == (s == 0):
+            k = [1024, 1280] if h == 0 else [1280, 1024]
+        elif mid:
+            k = [1280, 1280]
+        else:
+            k = [1024 + 256 * s] * 2
+        G(g.iota(T.li[:, o:o + 2], [[k[1] - k[0], 2]], k[0], 32, **fl))
+    if not outer:
+        G(g.iota(T.li[:, 8:9], [[1, 1]], 256 if bound else 512, 32, **fl))
     nconst = cg[0]
-    for b in ("cr", "sab", "dd", "ce", "co") + (("tt",) if mid else ()):
-        V(v.memset(T[b][:], 0.0))
-    v.wait_ge(S.gs, nconst)
-    V(v.tensor_scalar(T.pj[:], T.pi[:], 15, None, Op.bitwise_and))
-    V(v.tensor_scalar(T.p3[:], T.pi[:], 3, None, Op.bitwise_and))
-    vw()
-    V(v.tensor_copy(T.pp[:, 0:1], T.pj[:, 0:1]))
-    V(v.tensor_scalar(T.pp[:, 1:2], T.pj[:, 0:1], 16.0, None, Op.add))
-    if bound:
-        V(v.tensor_scalar(T.pp[:, 2:3], T.pj[:, 0:1], -512.0, None, Op.add))
-        V(v.tensor_scalar(T.pp[:, 3:4], T.pj[:, 0:1], -496.0, None, Op.add))
-    V(v.tensor_copy(T.of[:], T.p3[:]))
+    V(v.memset(T.cr[:], 0.0))
 
     g.wait_ge(S.sD, 32)
     ld = T["ld%d" % r]
 
-    def lists(ks, e, sem):
-        return RemoteDMATransfer(dst_ids=[dst(T.cores[k]) for k in ks], dma_engine_mask=1 << e, remote_sem=sem,
+    def lists(ks, e, sm):
+        return RemoteDMATransfer(dst_ids=[dst(T.cores[k]) for k in ks], dma_engine_mask=1 << e, remote_sem=sm,
                                  srcs=[T.d3[:]], dsts=[ld[:] for k in ks])
 
-    g.remote_dma_fused([lists([partner], on[0], S.lp), lists(far, off[0], S.lh), lists(other, off[2], S.lo)],
-                       local_sem=S.ls)
+    g.remote_dma_fused([lists([partner], on[0], S.lp), lists(far, off[0], S.lh),
+                        lists([k for k in other if r in ranks(k, (0, 1, 2))], off[2], S.lo)], local_sem=S.ls)
     cl[0] += 3
 
     m, n2 = r // 2, 2 * h
@@ -143,293 +176,367 @@ def rank_program(g, core, T, topo):
     v.wait_ge(S.own, 32)
     vw()
     V(v.tensor_tensor(T.cr[0:8, 0:1], o[0:8, 1, 0, m, m:m + 1], o[0:8, 0, 0, m, m:m + 1], Op.subtract))
-    if inner or third:
+    if hand:
         c = 4 + n2
         V(v.tensor_tensor(T.cr[0:8, 1:2], o[0:8, 0, 0, m, c:c + 1], o[0:8, 1, 0, m, c:c + 1], Op.subtract))
         V(v.tensor_tensor(T.cr[0:8, 2:3], o[0:8, 0, 0, m, c + 1:c + 2], o[0:8, 1, 0, m, c:c + 1], Op.subtract))
         V(v.tensor_tensor(T.cr[0:8, 3:4], o[0:8, 1, 0, m, c + 1:c + 2], o[0:8, 0, 0, m, c + 1:c + 2], Op.subtract))
     g.wait_ge(S.vs, cv[0])
-    if mid:
-        to, es, sem, src, place = partner, on, S.kp, T.cr[:, 0:1], T.cp[:]
-    elif third:
-        to, es, sem, src, place = land, off, S.kf, T.cr[:], T.cx[:]
-    else:
-        to, es, sem, src, place = land, off, S.kf, T.cr[:, 0:1], T.ck[:]
-    a = topo.addr(T.cores[to])
-    g.remote_dma(place, src, sem, S.ls, a[1], a[0], bits(es))
-    cl[0] += len(es)
+    n = 4 if hand else 1
+    to = [(land, off, S.kf, T["cx" if hand else "ck"])]
+    if not third:
+        to.append((partner, on, S.kp, T.cp))
+    g.remote_dma_fused([RemoteDMATransfer(dst_ids=[dst(T.cores[k])], dma_engine_mask=bits(es), remote_sem=sm,
+                                          srcs=[T.cr[:, 0:n]], dsts=[b[:, 0:n]]) for k, es, sm, b in to], local_sem=S.ls)
+    cl[0] += sum(len(x[1]) for x in to)
 
     c0 = block(r)
     v.wait_ge(S.wld, 16)
     nq = V(v.quantize_mx(T.hb[:, c0:c0 + 256], T.hbs[:, c0:c0 + 256], T.wt[:]))
-    V(v.quantize_mx(T.win[:, c0:c0 + 256], T.wins[:, c0:c0 + 256], T.wt[:]))
+    if outer:
+        V(v.quantize_mx(T.win[:, c0:c0 + 256], T.wins[:, c0:c0 + 256], T.wt[:]))
     g.wait_ge(S.vs, nq)
     for plane in (False, True):
-        src = T.hbs[:, c0:c0 + 256] if plane else T.hb[:, c0:c0 + 256].bitcast(dt.uint8)
-        g.remote_dma_fused([
-            RemoteDMATransfer(dst_ids=[dst(T.cores[partner])], dma_engine_mask=bits(on), remote_sem=S.bq if plane else S.bp,
-                              srcs=[src], dsts=[cols(partner, c0, 256, plane)]),
-            RemoteDMATransfer(dst_ids=[dst(T.cores[land])], dma_engine_mask=bits(off), remote_sem=S.bo,
-                              srcs=[src], dsts=[cols(land, c0, 256, plane)])], local_sem=S.ls)
+        g.remote_dma_fused([RemoteDMATransfer(dst_ids=[dst(T.cores[k])], dma_engine_mask=bits(es), remote_sem=sem(sm, plane),
+                                              srcs=[view("hb", c0, 256, plane)], dsts=[view(home_of_w(k, c0), c0, 256, plane)])
+                            for k, es, sm in ((partner, on, "bp"), (land, off, "bo"))], local_sem=S.ls)
         cl[0] += non + noff
-    v.wait_ge(S.xld, 16)
-    V(v.quantize_mx(T.xq[:, 0:512], T.xs[:, 0:512], T.xt[:, 0:2048]))
-    nx = V(v.quantize_mx(T.xq[:, 512:640], T.xs[:, 512:640], T.xt[:, 2048:2560]))
 
-    for hh in range(2):
-        for s, q in ((0, sy), (1, sc)):
-            for sem, n, js in ((S.lp, 1, [partner]), (S.lh, 2, far), (S.lo, 4, other)):
-                q.wait_ge(sem, n)
-                for j in js:
-                    a = 64 * hh + 32 * s
-                    q.dma_start(home(j, s, hh), T["ld%d" % j][a:a + 32, :]).then_inc(S.sP if hh else S.sO, 16)
-    nl = 16 * 2 * 7
-
-    def chip_there(q):
-        q.wait_ge(S.bp, non)
-        q.wait_ge(S.bq, non)
-
-    def half_there(q):
-        chip_there(q)
-        if inner or third:
-            q.wait_ge(S.bo, 4 * noff)
-        else:
-            q.wait_ge(S.br, 2 * (non if mid else len(near)))
-
-    def relay(src, c, w, sem, plane, es):
-        a = topo.addr(T.cores[partner])
-        to = T.wins[:, c:c + w] if plane else T.win[:, c:c + w].bitcast(dt.uint8)
-        g.remote_dma(to, src if src else to, sem, S.ls, a[1], a[0], bits(es))
+    def put(c, sb, a, db, b, w, sm, plane, es):
+        ad = topo.addr(c)
+        g.remote_dma(view(db, b, w, plane), view(sb, a, w, plane), sem(sm, plane), S.ls, ad[1], ad[0], bits(es))
         cl[0] += len(es)
 
-    def to_win(a, n):
-        sy.dma_start(T.win[:, a:a + n].bitcast(dt.uint8), T.hb[:, a:a + n].bitcast(dt.uint8)).then_inc(S.cw, 16)
-        sy.dma_start(T.wins[:, a:a + n], T.hbs[:, a:a + n]).then_inc(S.cw, 16)
-
     if mid:
-        chip_there(sy)
-        to_win(block(partner), 256)
-        if inner:
-            half_there(sy)
-            to_win(0, 512)
-    ncw = 64 if inner else 32
+        for plane in (False, True):
+            put(helper(r), "hb", c0, "hw", 0, 256, "hs", plane, on)
 
-    def send(k, x, sem, c, n1, n2):
-        a = topo.addr(T.cores[k])
-        g.wait_ge(S.vs, n1)
-        g.remote_dma(T.win[:, c:c + 256].bitcast(dt.uint8), T.pa[:, x:x + 256].bitcast(dt.uint8), sem, S.ls, a[1], a[0], bits(off))
-        g.wait_ge(S.ss, n2)
-        g.remote_dma(T.wins[:, c:c + 256], T.pas[:, x:x + 256], sem, S.ls, a[1], a[0], bits(off))
-        cl[0] += 2 * noff
+    for b in ("sab", "dd", "ce", "co") + (() if outer else ("tt",)):
+        V(v.memset(T[b][:], 0.0))
+    v.wait_ge(S.gs, nconst)
+    V(v.tensor_scalar(T.pj[:], T.pi[:], 15, None, Op.bitwise_and))
+    V(v.tensor_scalar(T.p3[:], T.pi[:], 3, None, Op.bitwise_and))
+    if mid:
+        V(v.tensor_scalar(T.ph[:], T.pi[:], 14, None, Op.bitwise_and))
+    vw()
+    V(v.tensor_copy(T.pp[:, 0:1], T.pj[:, 0:1]))
+    V(v.tensor_scalar(T.pp[:, 1:2], T.pj[:, 0:1], 16.0, None, Op.add))
+    if mid:
+        V(v.tensor_scalar(T.pp[:, 2:3], T.pj[:, 0:1], -512.0, None, Op.add))
+        V(v.tensor_scalar(T.pp[:, 3:4], T.pj[:, 0:1], -496.0, None, Op.add))
+        V(v.tensor_scalar(T.pf[:, 0:1], T.ph[:, 0:1], 0.0 if h else 2.0, 4.0, Op.is_equal, Op.mult))
+        V(v.tensor_copy(T.oz[:], T.p3[:]))
+        vw()
+        V(v.tensor_scalar(T.oz[:, 0:1], T.p3[:, 0:1], T.pf[:, 0:1], None, Op.add))
+    V(v.tensor_copy(T.of[:], T.p3[:]))
+    for s in range(2):
+        V(v.tensor_copy(T.sab[0:8, s, 0:4], T.li[0:8, 4 * s:4 * s + 4]))
 
-    def pick(x, wa, wb, fs, nlist, buf, src):
-        n1 = V(v.tensor_copy(T[buf][:, x:x + 256].bitcast(dt.uint32), T[src][:, wa:wb].bitcast(dt.uint32).indirect(fs)))
+    nx = [0]
+
+    def quantise_x():
+        v.wait_ge(S.xld, 16)
+        V(v.quantize_mx(T.xq[:, 0:512], T.xs[:, 0:512], T.xt[:, 0:2048]))
+        nx[0] = V(v.quantize_mx(T.xq[:, 512:640], T.xs[:, 512:640], T.xt[:, 2048:2560]))
+
+    if outer:
+        quantise_x()
+
+    cO, cP = [0], [0]
+    for s, q in ((0, sy), (1, sc)):
+        rest = []
+        for sm, js in ((S.lp, [partner]), (S.lh, list(far)), (S.lo, other)):
+            js = [j for j in js if j in ranks(r, (0, 1, 2))]
+            q.wait_ge(sm, len(js))
+            for j in js:
+                q.dma_start(home(j, s, 0), T["ld%d" % j][32 * s:32 * s + 32, :]).then_inc(S.sO, 16)
+                cO[0] += 16
+            rest += [j for j in js if j in ranks(r, (3, 4))]
+        for j in rest:
+            q.dma_start(home(j, s, 1), T["ld%d" % j][64 + 32 * s:96 + 32 * s, :]).then_inc(S.sP, 16)
+            cP[0] += 16
+
+    def chip_there(q, plane):
+        q.wait_ge(sem("bp", plane), non)
+
+    def half_there(q, plane):
+        chip_there(q, plane)
+        if hand:
+            q.wait_ge(sem("bo", plane), 2 * noff)
+        else:
+            q.wait_ge(sem("br", plane), non)
+
+    ncw = [0]
+
+    def to_win(a, n):
+        for plane in (False, True):
+            sy.dma_start(view("win", a, n, plane), view("hb", a, n, plane)).then_inc(S.cw, 16)
+            ncw[0] += 16
+
+    def pick(x, wa, wb, lt, nlist, buf, src, waits, w=256):
+        vw(nlist)
+        waits(v, False)
+        n1 = V(v.tensor_copy(T[buf][:, x:x + w].bitcast(dt.uint32), T[src][:, wa:wb].bitcast(dt.uint32).indirect(lt)))
         sc.wait_ge(S.vs, nlist)
-        return n1, A(sc.activation(T[buf + "s"][:, x:x + 256], T[src + "s"][:, wa:wb].indirect(fs), Act.Copy))
+        waits(sc, True)
+        return n1, A(sc.activation(T[buf + "s"][:, x:x + w], T[src + "s"][:, wa:wb].indirect(lt), Act.Copy))
 
     stat = {}
 
-    if mid:
+    if not outer:
         W = T.wk
         v.wait_ge(S.kp, non)
         vw()
-        pa, pb = (T.cp[0:8, :], T.cr[0:8, 0:1]) if r % 2 else (T.cr[0:8, 0:1], T.cp[0:8, :])
+        pa, pb = (T.cp[0:8, 0:1], T.cr[0:8, 0:1]) if r % 2 else (T.cr[0:8, 0:1], T.cp[0:8, 0:1])
         if bound:
             V(v.tensor_scalar(W[0:8, 2:3], pa, pb, -256.0, Op.is_gt, Op.mult))
             vw()
-            V(v.tensor_scalar(T.tt[0:8, 0:1], W[0:8, 2:3], T.li[0:8, 6:7], None, Op.add))
+            V(v.tensor_scalar(T.tt[0:8, 0:1], W[0:8, 2:3], T.li[0:8, 8:9], None, Op.add))
         else:
-            i = 4 if h else 5
+            i = 4 + m - n2
+            ii = 4 if h else 5
             V(v.tensor_tensor(W[0:8, i:i + 1], pa, pb, Op.is_gt))
             v.wait_ge(S.kf, 2 * noff)
-            fa, fb = (T.cx[0:8, 0:1], T.ck[0:8, :]) if h else (T.ck[0:8, :], T.cx[0:8, 0:1])
+            fa, fb = (T.cx[0:8, 0:1], T.ck[0:8, 0:1]) if min(far) in INNER + THIRD else (T.ck[0:8, 0:1], T.cx[0:8, 0:1])
             V(v.tensor_tensor(W[0:8, 9 - i:10 - i], fa, fb, Op.is_gt))
-            fa, fb = (T.cr[0:8, 1:4], T.cx[0:8, 1:4]) if h else (T.cx[0:8, 1:4], T.cr[0:8, 1:4])
+            fa, fb = (T.cr[0:8, 1:4], T.cx[0:8, 1:4]) if r % 2 else (T.cx[0:8, 1:4], T.cr[0:8, 1:4])
             V(v.tensor_tensor(W[0:8, 8:11], fa, fb, Op.subtract))
             vw()
-            V(v.tensor_scalar(W[0:8, 18:19], W[0:8, i:i + 1], 256.0, T.li[0:8, 6:7], Op.mult, Op.add))
-            V(v.tensor_tensor(W[0:8, 14:15], W[0:8, 8:9], W[0:8, 4:5], Op.mult))
-            V(v.tensor_scalar(W[0:8, 15:16], W[0:8, 10:11], W[0:8, 5:6], W[0:8, 9:10], Op.mult, Op.add))
             V(v.tensor_tensor(W[0:8, 16:17], W[0:8, 4:5], W[0:8, 5:6], Op.add))
-            vw()
+            V(v.tensor_tensor(W[0:8, 14:15], W[0:8, 8:9], W[0:8, 4:5], Op.mult))
+            n = V(v.tensor_scalar(W[0:8, 15:16], W[0:8, 10:11], W[0:8, 5:6], W[0:8, 9:10], Op.mult, Op.add))
+            V(v.tensor_scalar(W[0:8, 18:19], W[0:8, ii:ii + 1], 256.0, T.li[0:8, 8:9], Op.mult, Op.add))
+            vw(n)
             V(v.tensor_scalar(W[0:8, 17:18], W[0:8, 16:17], -256.0, -256.0, Op.mult, Op.add))
+            V(v.tensor_scalar(W[0:8, 20:21], W[0:8, 15:16], W[0:8, 14:15], None, Op.is_gt))
             vw()
-            V(v.tensor_scalar(W[0:8, 19:20], W[0:8, 15:16], W[0:8, 14:15], W[0:8, 17:18], Op.is_gt, Op.mult))
-            vw()
-            V(v.tensor_scalar(T.tt[0:8, 0:1], W[0:8, 19:20], W[0:8, 18:19], None, Op.add))
+            V(v.tensor_scalar(T.tt[0:8, 0:1], W[0:8, 20:21], W[0:8, 17:18], W[0:8, 18:19], Op.mult, Op.add))
         vw()
         n = V(v.transpose(T.tr[0:32, :], T.tt[0:32, :]))
         g.wait_ge(S.vs, n)
         n = G(g.partition_broadcast(T.bj[:], T.tr[0:1, 0:8], 128))
         v.wait_ge(S.gs, n)
         V(v.tensor_scalar(T.jl[:, 0:16:2], T.bj[:], T.pp[:, 0:1], None, Op.add))
-        n = V(v.tensor_scalar(T.jl[:, 1:16:2], T.bj[:], T.pp[:, 1:2], None, Op.add))
-        vw()
-        for q in (v, sc):
-            (chip_there if bound else half_there)(q)
+        njl = V(v.tensor_scalar(T.jl[:, 1:16:2], T.bj[:], T.pp[:, 1:2], None, Op.add))
         if bound:
-            n1, n2 = pick(0, 512, 1024, T.jl[:], n, "pa", "hb")
-            stat[0] = ("pa", 0, n1, n2)
-            for k in ((4, 6) if h == 0 else (3, 1)):
-                send(k, 0, S.x1, 1024, n1, n2)
-        else:
-            n1, n2 = pick(256, 0, 1024, T.jl[:], n, "pa", "hb")
-            stat[1] = ("pa", 256, n1, n2)
-            to = (4, 5) if h == 0 else (3, 2)
-            half_there(g)
-            relay(T.hb[:, 0:512].bitcast(dt.uint8), 0, 512, S.br, False, on)
-            send(to[0], 256, S.x2, 1280, n1, n2)
-            relay(T.hbs[:, 0:512], 0, 512, S.br, True, on)
-            send(to[1], 256, S.x2, 1280, n1, n2)
+            n1, n2_ = pick(0, 512, 1024, T.jl[:], njl, "pa", "hb", chip_there)
+            stat[0] = ("pa", 0, n1, n2_)
+            g.wait_ge(S.vs, n1)
+            put(T.cores[7 - r], "pa", 0, "win", 1024, 256, "x1", False, off)
+            g.wait_ge(S.ss, n2_)
+            put(T.cores[7 - r], "pa", 0, "win", 1024, 256, "x1", True, off)
+        quantise_x()
 
-    if third:
-        half_there(g)
+    def send_x2():
+        x = 256 if inner else 768
+        n1, n2_ = pick(x, 0, 1024, T.jl[:], njl, "pa", "hb", half_there)
+        if inner:
+            stat[1] = ("pa", x, n1, n2_)
+        for plane, n in ((False, n1), (True, n2_)):
+            g.wait_ge(S.ss if plane else S.vs, n)
+            put(T.cores[X2_TO[r]], "pa", x, "win", 1280, 256, "x2", plane, off)
+
+    if hand:
+        fc = 0 if inner else 512
         for plane in (False, True):
-            relay(None, 512, 512, S.br, plane, near)
+            half_there(g, plane)
+            put(T.cores[partner], "hb", fc, "win", fc, 512, "br", plane, on)
+        if inner:
+            send_x2()
+
+    PR = [pairs(r, t) for t in range(5)]
+    COL, e = {}, 4
+    for t in (4, 3, 2, 1):
+        COL[t] = e
+        e += 4 * len(PR[t])
+    SIZE = [e, COL[1], COL[2], COL[3], 4]
 
     def numbers(t):
         hh, f = TI[t]
+        a, b = PR[t][0], PR[t][-1] + 1
+        to = T.sab[0:8, :, COL[t]:COL[t] + 4 * (b - a)] if t else T.e0[0:8, :, 0:4 * (b - a)]
         if t % 2 == 0:
-            to = T.sab[0:8, :, COL[t]:COL[t] + 16] if t else T.e0[0:8, :, :]
-            V(v.tensor_tensor(to, T.se[0:8, :, hh, :, f:f + 4], T.so[0:8, :, hh, :, f:f + 4], Op.subtract))
+            V(v.tensor_tensor(to, T.se[0:8, :, hh, a:b, f:f + 4], T.so[0:8, :, hh, a:b, f:f + 4], Op.subtract))
         else:
-            V(v.tensor_tensor(T.sab[0:8, :, COL[t]:COL[t] + 12], T.so[0:8, :, hh, 0:3, f:f + 4],
-                              T.se[0:8, :, hh, 1:4, f:f + 4], Op.subtract))
+            V(v.tensor_tensor(to, T.so[0:8, :, hh, a:b, f:f + 4], T.se[0:8, :, hh, a + 1:b + 1, f:f + 4], Op.subtract))
 
     level = [0] * 8
     need = []
-    nlist = {}
-    for s in range(2):
-        V(v.tensor_copy(T.sab[0:8, s, 2 * h:2 * h + 2], T.li[0:8, 2 * s:2 * s + 2]))
-    v.wait_ge(S.own, 32)
-    v.wait_ge(S.sO, nl)
-    for t in range(3):
-        numbers(t)
-    v.wait_ge(S.ow2, 32)
-    v.wait_ge(S.sP, nl)
-    for t in (3, 4):
-        numbers(t)
-
-    t0 = 1 if bound else 0
-    first, groups = range(t0, 1 if inner else 2), []
     for t in range(5):
-        n = SIZE[t]
-        odd = t % 2
-        vw()
-        if not odd:
-            a, b = T.sab[0:8, 0, 0:n], T.sab[0:8, 1, 0:n]
-            if t == 0:
-                ea, eb = T.e0[0:8, 0, 0:16:5], T.e0[0:8, 1, 0:16:5]
-            else:
-                c = COL[t]
-                ea, eb = T.sab[0:8, 0, c:c + 16:5], T.sab[0:8, 1, c:c + 16:5]
-            cc, np = T.ce, 4
-        else:
-            a, b = T.sab[0:8, 1, 0:n], T.sab[0:8, 0, 1:n + 1]
-            c = COL[t]
-            ea, eb = T.sab[0:8, 1, c:c + 11:5], T.sab[0:8, 0, c + 1:c + 12:5]
-            cc, np = T.co, 3
-        V(v.tensor_tensor(cc[0:8, 0:np], eb, ea, Op.is_gt))
-        V(v.tensor_tensor(T.dd[0:8, 0:n], b, a, Op.subtract))
-        vw()
-        V(v.tensor_tensor(T.cd[:, 0:n], cc[:, 0:8].indirect(T.of[:, 0:n // 16]), T.dd[:, 0:n], Op.mult))
-        vw()
-        V(v.tensor_tensor(a, a, T.cd[0:8, 0:n], Op.add))
-        V(v.tensor_tensor(b, b, T.cd[0:8, 0:n], Op.subtract))
-        for k in range(odd, 7, 2):
+        for k in range(t % 2, 7, 2):
             level[k] = level[k + 1] = max(level[k], level[k + 1])
         if t < 2:
-            pos = (4 + t) if h == 0 else (3 - t)
-            vw()
-            V(v.tensor_copy(T.sab[0:8, pos % 2, pos // 2:pos // 2 + 1], T.li[0:8, 4 + t:5 + t]))
-            level[pos] = 1 + t
+            level[(4 + t) if h == 0 else (3 - t)] = 1 + t
         need.append(level[r])
-        if t > 1 or t in first:
-            vw()
-            k = V(v.transpose(T.tf[0:32, 8 * t:8 * t + 32], T.sab[0:32, r % 2, r // 2:r // 2 + 32]))
-        if t == first[-1] or t == 4:
-            t0 = first[0] if t < 2 else 2
-            g.wait_ge(S.vs, k)
-            groups.append((t0, t + 1, G(g.partition_broadcast(T.bf[0:128, 8 * t0:8 * t + 8], T.tf[0:1, 8 * t0:8 * t + 8], 128))))
-    for t0, t1, k in groups:
+
+    def ready(t):
+        lv = need[t]
+        if hand and t == 0:
+            return "pa", "hb", 512 if inner else 0, 1024 if inner else 512, chip_there
+        if third and t < 3:
+            return "pa", "hb", 0, 1024, half_there
+        if outer and t < 2:
+            return "pk", "win", 0, 512, chip_there
+
+        def waits(q, plane):
+            if bound and t == 1:
+                chip_there(q, plane)
+            else:
+                half_there(q, plane)
+            if not outer:
+                q.wait_ge(S.cw, ncw[0])
+            if mid:
+                if lv >= 1:
+                    q.wait_ge(sem("x1", plane), nx1)
+                if lv >= 2:
+                    q.wait_ge(sem("x2", plane), noff)
+            elif lv:
+                q.wait_ge(sem("rw", plane), 2 * noff)
+        if bound and t == 1:
+            return "pk", "win", 512, 1280, waits
+        return "pk", "win", 0, 1024 + (256 * lv if mid else 512 * lv), waits
+
+    nlist = {}
+
+    def make_lists(t0, t1, k, shift=False):
         v.wait_ge(S.gs, k)
         fr = T.bf[:, 8 * t0:8 * t1]
-        o = 2 if bound and t1 == 2 else 0
+        o = 2 if shift else 0
         V(v.tensor_scalar(T.lu[:, 16 * t0:16 * t1:2], fr, T.pp[:, o:o + 1], None, Op.add))
         n = V(v.tensor_scalar(T.lu[:, 16 * t0 + 1:16 * t1:2], fr, T.pp[:, o + 1:o + 2], None, Op.add))
         for t in range(t0, t1):
             nlist[t] = n
 
-    if bound or third:
-        g.wait_ge(S.x1, 2 * noff)
-        for plane in (False, True):
-            relay(None, 1024, 256, S.x1, plane, near)
+    def do_pick(t):
+        buf, src, wa, wb, waits = ready(t)
+        n1, n2_ = pick(256 * t, wa, wb, T.lu[:, 16 * t:16 * t + 16], nlist[t], buf, src, waits)
+        stat[t] = (buf, 256 * t, n1, n2_)
+
+    v.wait_ge(S.own, 32)
+    v.wait_ge(S.sO, cO[0])
+    for t in range(3):
+        numbers(t)
+    v.wait_ge(S.ow2, 32)
+    v.wait_ge(S.sP, cP[0])
+    for t in (3, 4):
+        numbers(t)
+
+    f0, f1 = (1, 2) if bound else (0, 1) if inner else (0, 2)
+    groups = {f1 - 1: (f0, f1), 3: (2, 4), 4: (4, 5)}
+    pb, last = {}, cv[0]
+
+    def turn(t):
+        if t < f0 or f1 <= t < 2:
+            return
+        k = V(v.transpose(T.tf[0:32, 8 * t:8 * t + 32], T.sab[0:32, r % 2, m:m + 32]))
+        if t in groups:
+            a, b = groups[t]
+            g.wait_ge(S.vs, k)
+            pb[t] = G(g.partition_broadcast(T.bf[0:128, 8 * a:8 * b], T.tf[0:1, 8 * a:8 * b], 128))
+            if bound and t < 4:
+                plane = t > 1
+                g.wait_ge(sem("x1", plane), noff)
+                put(T.cores[partner], "win", 1024, "win", 1024, 256, "x1", plane, near)
+
+    for t in range(5):
+        n, odd = SIZE[t], t % 2
+        n16 = -(-n // 16)
+        lo, np = PR[t][0], len(PR[t])
+        a, b = (T.sab[0:8, 1, 0:n], T.sab[0:8, 0, 1:n + 1]) if odd else (T.sab[0:8, 0, 0:n], T.sab[0:8, 1, 0:n])
+        eb, c = (T.sab, COL[t] + lo) if t else (T.e0, lo)
+        w = 5 * np - 4
+        ea, eb = eb[0:8, odd, c:c + w:5], eb[0:8, 1 - odd, c + odd:c + odd + w:5]
+        cc = T.co if odd else T.ce
+        vw(last)
+        V(v.tensor_tensor(cc[0:8, lo:lo + np], eb, ea, Op.is_gt))
+        k = V(v.tensor_tensor(T.dd[0:8, 0:n], b, a, Op.subtract))
+        if t:
+            turn(t - 1)
+        vw(k)
+        of = T.oz if mid and t == 0 else T.of
+        k = V(v.tensor_tensor(T.cd[:, 0:16 * n16], cc[:, 0:8].indirect(of[:, 0:n16]), T.dd[:, 0:16 * n16], Op.mult))
+        if t == 3:
+            make_lists(f0, f1, pb[f1 - 1], mid)
+        vw(k)
+        V(v.tensor_tensor(a, a, T.cd[0:8, 0:n], Op.add))
+        last = V(v.tensor_tensor(b, b, T.cd[0:8, 0:n], Op.subtract))
+        if t == 0 and not outer:
+            sy.wait_ge(S.vs, last if bound else nq)
+            for plane in (False, True):
+                (half_there if hand else chip_there)(sy, plane)
+            to_win(512 if bound else 0, 512 if bound else 1024)
+        if third and t == 2:
+            send_x2()
+        if t == 3 and not bound:
+            do_pick(0)
+    vw(last)
+    turn(4)
 
     copied = {}
-    nx1 = 2 * (noff if bound or third else len(near))
-
-    def ready(q, t, lv):
-        if inner and t == 0:
-            half_there(q)
-            return "pa", "hb", 0, 1024
-        if mid:
-            q.wait_ge(S.cw, ncw)
-        if lv >= 1:
-            q.wait_ge(S.x1, nx1)
-        if lv >= 2:
-            q.wait_ge(S.x2, 2 * noff)
-        if bound and t == 1:
-            return "pk", "win", 512, 1280
-        if not mid and t < (1 if third else 2):
-            chip_there(q)
-            return "pk", "win", 0, 512
-        half_there(q)
-        return "pk", "win", 0, 1024 + 256 * lv
+    VB = (2, 3) if inner else (2,)
 
     def out(t):
         o = 256 * t
         e = [512 * ((2 * t + k) % 8) for k in range(2)]
         v.wait_ge(S.ps, 2 * t + 1)
         n1 = V(v.tensor_copy(T.ys[:, o:o + 128], T.acc[:, e[0]:e[0] + 128]))
-        sc.wait_ge(S.ps, 2 * t + 2)
-        n2 = A(sc.activation(T.ys[:, o + 128:o + 256], T.acc[:, e[1]:e[1] + 128], Act.Copy))
-        copied[t] = (n1, n2)
+        if t in VB:
+            v.wait_ge(S.ps, 2 * t + 2)
+            n1 = V(v.tensor_copy(T.ys[:, o + 128:o + 256], T.acc[:, e[1]:e[1] + 128]))
+            n2_ = 0
+        else:
+            sc.wait_ge(S.ps, 2 * t + 2)
+            n2_ = A(sc.activation(T.ys[:, o + 128:o + 256], T.acc[:, e[1]:e[1] + 128], Act.Copy))
+        copied[t] = (n1, n2_)
         sy.wait_ge(S.vs, n1)
         if t < 4:
-            sy.wait_ge(S.ss, n2)
+            if n2_:
+                sy.wait_ge(S.ss, n2_)
             sy.dma_start(T.y[:, o:o + 256], T.ys[:, o:o + 256]).then_inc(S.st, 16)
             cst[0] += 16
         else:
             sy.dma_start(T.y[:, o:o + 128], T.ys[:, o:o + 128]).then_inc(S.st, 16)
-            sc.wait_ge(S.ss, n2)
+            sc.wait_ge(S.ss, n2_)
             sc.dma_start(T.y[:, o + 128:o + 256], T.ys[:, o + 128:o + 256]).then_inc(S.st, 16)
             cst[0] += 32
 
-    for t in range(5):
-        if t not in stat:
-            vw()
-            for q in (v, sc):
-                buf, src, wa, wb = ready(q, t, need[t])
-            n1, n2 = pick(256 * t, wa, wb, T.lu[:, 16 * t:16 * t + 16], nlist[t], buf, src)
-            stat[t] = (buf, 256 * t, n1, n2)
-        buf, x, n1, n2 = stat[t]
-        te.wait_ge(S.vs, max(n1, nx))
-        te.wait_ge(S.ss, n2)
+    def product(t, ks=(0, 1)):
+        buf, x, n1, n2_ = stat[t]
+        te.wait_ge(S.vs, max(n1, nx[0]))
+        te.wait_ge(S.ss, n2_)
         if t == 4:
             te.wait_ge(S.vs, copied[0][0])
             te.wait_ge(S.ss, copied[0][1])
-        for k in range(2):
+        for k in ks:
             e = 512 * ((2 * t + k) % 8)
             c = x + 128 * k
             te.matmul_mx(T.acc[:, e:e + 128], T[buf][:, c:c + 128], T[buf + "s"][:, c:c + 128],
                          T.xq[:, 128 * t:128 * t + 128], T.xs[:, 128 * t:128 * t + 128], True, True).then_inc(S.ps, 1)
-        if t > 0:
+
+    for t in range(5):
+        if inner and t == 2:
+            out(1)
+        if t in (2, 4):
+            make_lists(t, min(5, t + 2), pb[4 if t == 4 else 3])
+        if t not in stat and t < 4:
+            do_pick(t)
+        if t < 4:
+            product(t)
+        else:
+            buf, src, wa, wb, waits = ready(t)
+            for k in range(2):
+                n1, n2_ = pick(256 * t + 128 * k, wa, wb, T.lu[:, 16 * t + 8 * k:16 * t + 8 * k + 8], nlist[t], buf, src,
+                               waits, 128)
+                stat[t] = (buf, 256 * t, n1, n2_)
+                product(t, (k,))
+        if t > 0 and (t != 2 or not inner):
             out(t - 1)
     out(4)
 
-    v.wait_ge(S.x1, nx1)
-    if mid:
-        v.wait_ge(S.x2, 2 * noff)
+    for plane in (False, True):
+        half_there(v, plane)
+        for name, n in (("x1", nx1), ("x2", noff)) if mid else (("rw", 2 * noff),):
+            v.wait_ge(sem(name, plane), n)
     vw()
     sc.wait_ge(S.ss, cs[0])
     te.wait_ge(S.ps, 10)

from concourse.bass import DstId, RemoteDMATransfer
from concourse.mybir import dt, AluOpType as Op, ActivationFunctionType as Act

C8 = "float8_e4m3fn_x4"
SCRATCH = {
    "d3": ("dram", [128, 3], "int32"),
    "wt": ("sbuf", [128, 1024], "bfloat16"),
    "xt": ("sbuf", [128, 2560], "bfloat16"),
    "xq": ("sbuf", [128, 640], C8), "xs": ("sbuf", [128, 640], "uint8"),
    "hb": ("sbuf", [128, 1024], C8), "hbs": ("sbuf", [128, 1024], "uint8"),
    "win": ("sbuf", [128, 1536], C8), "wins": ("sbuf", [128, 1536], "uint8"),
    "pa": ("sbuf", [128, 1024], C8), "pas": ("sbuf", [128, 1024], "uint8"),
    "hw": ("sbuf", [128, 256], C8), "hws": ("sbuf", [128, 256], "uint8"),
    "pk": ("sbuf", [128, 1280], C8), "pks": ("sbuf", [128, 1280], "uint8"),
    "se": ("sbuf", [128, 2, 2, 4, 12], "int32"), "so": ("sbuf", [128, 2, 2, 4, 12], "int32"),
    "cr": ("sbuf", [128, 4], "float32"),
    "cp": ("sbuf", [128, 4], "float32"), "ck": ("sbuf", [128, 4], "float32"), "cx": ("sbuf", [128, 4], "float32"),
    "sab": ("sbuf", [128, 2, 68], "float32"),
    "e0": ("sbuf", [128, 2, 16], "float32"),
    "dd": ("sbuf", [128, 64], "float32"), "cd": ("sbuf", [128, 64], "float32"),
    "ce": ("sbuf", [128, 8], "float32"), "co": ("sbuf", [128, 8], "float32"),
    "wk": ("sbuf", [128, 32], "float32"),
    "li": ("sbuf", [128, 12], "float32"), "pp": ("sbuf", [128, 4], "float32"),
    "pi": ("sbuf", [128, 4], "int32"), "pj": ("sbuf", [128, 4], "int32"), "p3": ("sbuf", [128, 4], "int32"),
    "ph": ("sbuf", [128, 4], "int32"), "pf": ("sbuf", [128, 2], "float32"),
    "of": ("sbuf", [128, 4], "uint16"), "oz": ("sbuf", [128, 4], "uint16"),
    "tt": ("sbuf", [128, 32], "float32"), "tr": ("sbuf", [128, 32], "float32"),
    "bj": ("sbuf", [128, 8], "float32"), "jl": ("sbuf", [128, 16], "uint16"),
    "tf": ("sbuf", [128, 64], "float32"), "bf": ("sbuf", [128, 40], "float32"), "lu": ("sbuf", [128, 80], "uint16"),
    "ys": ("sbuf", [128, 1280], "float32"),
    "acc": ("psum", [128, 4096], "float32"),
}
for _j in range(8):
    SCRATCH["ld%d" % _j] = ("dram", [128, 3], "int32")
SEMAPHORES = ["sD", "wld", "xld", "own", "ow2", "lp", "lh", "lo", "kp", "kf", "sO", "sP", "bp", "bps", "bo", "bos", "br", "brs",
              "x1", "x1s", "x2", "x2s", "rw", "rws", "hs", "hss", "cw", "vs", "gs", "ss", "ps", "st", "ls"]

TI = [(0, 0), (0, 4), (0, 8), (1, 4), (1, 8)]
OUTER, THIRD, INNER, BOUND = (0, 7), (1, 6), (2, 5), (3, 4)
OUTSIDE = {2: 6, 3: 7, 4: 0, 5: 1}
X2_TO = {2: 4, 1: 5, 5: 3, 6: 2}


def block(r):
    return 256 * min(r, 7 - r)


def pairs(r, t):
    m = r // 2
    d = (5 - t) // 2
    return list(range(max(0, m - d), min(2, m + d - 1) + 1)) if t % 2 else list(range(max(0, m - d), min(3, m + d) + 1))


def ranks(r, ts):
    return sorted({2 * k + t % 2 + i for t in ts for k in pairs(r, t) for i in range(2)})


def rank_program(g, core, T, topo):
    S = T.sem
    r = T.rank_of(core)

    def dst(c):
        a = topo.addr(c)
        return DstId(rid=a[0], pnc=a[1])

    def bits(es):
        return sum(1 << e for e in es)

    def sem(name, plane):
        return S[name + ("s" if plane else "")]

    def view(b, c, n, plane):
        return T[b + "s"][:, c:c + n] if plane else T[b][:, c:c + n].bitcast(dt.uint8)

    def helper(k):
        c, to = T.cores[k], T.cores[OUTSIDE[k]]
        return [x for x in topo.cores_of(c) if x not in T.cores and (topo.die(x) == topo.die(c)) == (k % 2 == 1)
                and topo.may_write(x, to)][0]

    if r is None:
        for k in INNER + BOUND:
            if core == helper(k):
                to = sorted([OUTSIDE[k], OUTSIDE[k] ^ 1], key=lambda j: j in OUTER)
                es = topo.engines(core, T.cores[to[0]])
                n = len([e for e in topo.engines(T.cores[k], core) if e not in es])
                for plane in (False, True):
                    g.wait_ge(sem("hs", plane), n)
                    g.remote_dma_fused([RemoteDMATransfer(
                        dst_ids=[dst(T.cores[j]) for j in to], dma_engine_mask=bits(es), remote_sem=sem("rw", plane),
                        srcs=[view("hw", 0, 256, plane)],
                        dsts=[view("win", 1024 + 256 * (k % 2), 256, plane) for j in to])], local_sem=S.ls)
                g.wait_ge(S.ls, 2 * len(es))
        return

    v, sc, sy, te = g.vector, g.scalar, g.sync, g.tensor
    h = r // 4
    bound, inner, third, outer = r in BOUND, r in INNER, r in THIRD, r in OUTER
    mid = bound or inner
    hand = inner or third
    cv, cg, cs, cl, cst = [0], [0], [0], [0], [0]

    def V(i):
        i.then_inc(S.vs, 1)
        cv[0] += 1
        return cv[0]

    def vw(n=None):
        v.wait_ge(S.vs, n or cv[0])

    def G(i):
        i.then_inc(S.gs, 1)
        cg[0] += 1
        return cg[0]

    def A(i):
        i.then_inc(S.ss, 1)
        cs[0] += 1
        return cs[0]

    def home_of_w(k, c):
        return "hb" if k in INNER + THIRD or (k in BOUND and c >= 512) else "win"

    partner = r ^ 1
    far = [(2, 3), (0, 1), (7, 6), (5, 4)][r // 2]
    land = [j for j in far if j in INNER + THIRD][0]
    other = [k for k in range(8) if k // 4 != h]
    near = topo.engines(core, T.cores[partner])
    off = topo.engines(core, T.cores[land])
    on = [e for e in near if e not in off]
    non, noff, nall = len(on), len(off), len(near)
    nx1 = noff if bound else nall

    def home(j, s, hh):
        return T["so" if j % 2 else "se"][0:8, s, hh, j // 2, :]

    sy.dma_start(T.d3[0:64, :], T.dm[:, 0:12]).then_inc(S.sD, 16)
    sc.dma_start(T.d3[64:128, :], T.dm[:, 8:20]).then_inc(S.sD, 16)
    for hh in range(2):
        for s, q in ((0, sy), (1, sc)):
            q.dma_start(home(r, s, hh), T.dm[8 * s:8 * s + 8, 8 * hh:8 * hh + 12]).then_inc(S.ow2 if hh else S.own, 16)
        if hh == 0:
            sy.dma_start(T.wt[:], T.w[:]).then_inc(S.wld, 16)
    sy.dma_start(T.xt[:], T.x[:]).then_inc(S.xld, 16)

    G(g.iota(T.pi[:], [[0, 4]], 0, 1))
    fl = dict(allow_small_or_imprecise_dtypes=True)
    for s in range(2):
        b = block(4 * h + s)
        G(g.iota(T.li[:, 4 * s + 2 * h:4 * s + 2 * h + 2], [[block(4 * h + s + 2) - b, 2]], b, 32, **fl))
        o = 4 * s + 2 * (1 - h)
        if mid and (h == 0) == (s == 0):
            k = [1024, 1280] if h == 0 else [1280, 1024]
        elif mid:
            k = [1280, 1280]
        else:
            k = [1024 + 256 * s] * 2
        G(g.iota(T.li[:, o:o + 2], [[k[1] - k[0], 2]], k[0], 32, **fl))
    if not outer:
        G(g.iota(T.li[:, 8:9], [[1, 1]], 256 if bound else 512, 32, **fl))
    nconst = cg[0]
    V(v.memset(T.cr[:], 0.0))

    g.wait_ge(S.sD, 32)
    ld = T["ld%d" % r]

    def lists(ks, e, sm):
        return RemoteDMATransfer(dst_ids=[dst(T.cores[k]) for k in ks], dma_engine_mask=1 << e, remote_sem=sm,
                                 srcs=[T.d3[:]], dsts=[ld[:] for k in ks])

    g.remote_dma_fused([lists([partner], on[0], S.lp), lists(far, off[0], S.lh),
                        lists([k for k in other if r in ranks(k, (0, 1, 2))], off[2], S.lo)], local_sem=S.ls)
    cl[0] += 3

    m, n2 = r // 2, 2 * h
    o = T.so if r % 2 else T.se
    v.wait_ge(S.own, 32)
    vw()
    V(v.tensor_tensor(T.cr[0:8, 0:1], o[0:8, 1, 0, m, m:m + 1], o[0:8, 0, 0, m, m:m + 1], Op.subtract))
    if hand:
        c = 4 + n2
        V(v.tensor_tensor(T.cr[0:8, 1:2], o[0:8, 0, 0, m, c:c + 1], o[0:8, 1, 0, m, c:c + 1], Op.subtract))
        V(v.tensor_tensor(T.cr[0:8, 2:3], o[0:8, 0, 0, m, c + 1:c + 2], o[0:8, 1, 0, m, c:c + 1], Op.subtract))
        V(v.tensor_tensor(T.cr[0:8, 3:4], o[0:8, 1, 0, m, c + 1:c + 2], o[0:8, 0, 0, m, c + 1:c + 2], Op.subtract))
    g.wait_ge(S.vs, cv[0])
    n = 4 if hand else 1
    to = [(land, off, S.kf, T["cx" if hand else "ck"])]
    if not third:
        to.append((partner, on, S.kp, T.cp))
    g.remote_dma_fused([RemoteDMATransfer(dst_ids=[dst(T.cores[k])], dma_engine_mask=bits(es), remote_sem=sm,
                                          srcs=[T.cr[:, 0:n]], dsts=[b[:, 0:n]]) for k, es, sm, b in to], local_sem=S.ls)
    cl[0] += sum(len(x[1]) for x in to)

    c0 = block(r)
    v.wait_ge(S.wld, 16)
    nq = V(v.quantize_mx(T.hb[:, c0:c0 + 256], T.hbs[:, c0:c0 + 256], T.wt[:]))
    if outer:
        V(v.quantize_mx(T.win[:, c0:c0 + 256], T.wins[:, c0:c0 + 256], T.wt[:]))
    g.wait_ge(S.vs, nq)
    for plane in (False, True):
        g.remote_dma_fused([RemoteDMATransfer(dst_ids=[dst(T.cores[k])], dma_engine_mask=bits(es), remote_sem=sem(sm, plane),
                                              srcs=[view("hb", c0, 256, plane)], dsts=[view(home_of_w(k, c0), c0, 256, plane)])
                            for k, es, sm in ((partner, on, "bp"), (land, off, "bo"))], local_sem=S.ls)
        cl[0] += non + noff

    def put(c, sb, a, db, b, w, sm, plane, es):
        ad = topo.addr(c)
        g.remote_dma(view(db, b, w, plane), view(sb, a, w, plane), sem(sm, plane), S.ls, ad[1], ad[0], bits(es))
        cl[0] += len(es)

    if mid:
        for plane in (False, True):
            put(helper(r), "hb", c0, "hw", 0, 256, "hs", plane, on)

    for b in ("sab", "dd", "ce", "co") + (() if outer else ("tt",)):
        V(v.memset(T[b][:], 0.0))
    v.wait_ge(S.gs, nconst)
    V(v.tensor_scalar(T.pj[:], T.pi[:], 15, None, Op.bitwise_and))
    V(v.tensor_scalar(T.p3[:], T.pi[:], 3, None, Op.bitwise_and))
    if mid:
        V(v.tensor_scalar(T.ph[:], T.pi[:], 14, None, Op.bitwise_and))
    vw()
    V(v.tensor_copy(T.pp[:, 0:1], T.pj[:, 0:1]))
    V(v.tensor_scalar(T.pp[:, 1:2], T.pj[:, 0:1], 16.0, None, Op.add))
    if mid:
        V(v.tensor_scalar(T.pp[:, 2:3], T.pj[:, 0:1], -512.0, None, Op.add))
        V(v.tensor_scalar(T.pp[:, 3:4], T.pj[:, 0:1], -496.0, None, Op.add))
        V(v.tensor_scalar(T.pf[:, 0:1], T.ph[:, 0:1], 0.0 if h else 2.0, 4.0, Op.is_equal, Op.mult))
        V(v.tensor_copy(T.oz[:], T.p3[:]))
        vw()
        V(v.tensor_scalar(T.oz[:, 0:1], T.p3[:, 0:1], T.pf[:, 0:1], None, Op.add))
    V(v.tensor_copy(T.of[:], T.p3[:]))
    for s in range(2):
        V(v.tensor_copy(T.sab[0:8, s, 0:4], T.li[0:8, 4 * s:4 * s + 4]))

    nx = [0]

    def quantise_x():
        v.wait_ge(S.xld, 16)
        V(v.quantize_mx(T.xq[:, 0:512], T.xs[:, 0:512], T.xt[:, 0:2048]))
        nx[0] = V(v.quantize_mx(T.xq[:, 512:640], T.xs[:, 512:640], T.xt[:, 2048:2560]))

    if outer:
        quantise_x()

    cO, cP = [0], [0]
    for s, q in ((0, sy), (1, sc)):
        rest = []
        for sm, js in ((S.lp, [partner]), (S.lh, list(far)), (S.lo, other)):
            js = [j for j in js if j in ranks(r, (0, 1, 2))]
            q.wait_ge(sm, len(js))
            for j in js:
                q.dma_start(home(j, s, 0), T["ld%d" % j][32 * s:32 * s + 32, :]).then_inc(S.sO, 16)
                cO[0] += 16
            rest += [j for j in js if j in ranks(r, (3, 4))]
        for j in rest:
            q.dma_start(home(j, s, 1), T["ld%d" % j][64 + 32 * s:96 + 32 * s, :]).then_inc(S.sP, 16)
            cP[0] += 16

    def chip_there(q, plane):
        q.wait_ge(sem("bp", plane), non)

    def half_there(q, plane):
        chip_there(q, plane)
        if hand:
            q.wait_ge(sem("bo", plane), 2 * noff)
        else:
            q.wait_ge(sem("br", plane), non)

    ncw = [0]

    def to_win(a, n):
        for plane in (False, True):
            sy.dma_start(view("win", a, n, plane), view("hb", a, n, plane)).then_inc(S.cw, 16)
            ncw[0] += 16

    def pick(x, wa, wb, lt, nlist, buf, src, waits, w=256):
        vw(nlist)
        waits(v, False)
        n1 = V(v.tensor_copy(T[buf][:, x:x + w].bitcast(dt.uint32), T[src][:, wa:wb].bitcast(dt.uint32).indirect(lt)))
        sc.wait_ge(S.vs, nlist)
        waits(sc, True)
        return n1, A(sc.activation(T[buf + "s"][:, x:x + w], T[src + "s"][:, wa:wb].indirect(lt), Act.Copy))

    stat = {}

    if not outer:
        W = T.wk
        v.wait_ge(S.kp, non)
        vw()
        pa, pb = (T.cp[0:8, 0:1], T.cr[0:8, 0:1]) if r % 2 else (T.cr[0:8, 0:1], T.cp[0:8, 0:1])
        if bound:
            V(v.tensor_scalar(W[0:8, 2:3], pa, pb, -256.0, Op.is_gt, Op.mult))
            vw()
            V(v.tensor_scalar(T.tt[0:8, 0:1], W[0:8, 2:3], T.li[0:8, 8:9], None, Op.add))
        else:
            i = 4 + m - n2
            ii = 4 if h else 5
            V(v.tensor_tensor(W[0:8, i:i + 1], pa, pb, Op.is_gt))
            v.wait_ge(S.kf, 2 * noff)
            fa, fb = (T.cx[0:8, 0:1], T.ck[0:8, 0:1]) if min(far) in INNER + THIRD else (T.ck[0:8, 0:1], T.cx[0:8, 0:1])
            V(v.tensor_tensor(W[0:8, 9 - i:10 - i], fa, fb, Op.is_gt))
            fa, fb = (T.cr[0:8, 1:4], T.cx[0:8, 1:4]) if r % 2 else (T.cx[0:8, 1:4], T.cr[0:8, 1:4])
            V(v.tensor_tensor(W[0:8, 8:11], fa, fb, Op.subtract))
            vw()
            V(v.tensor_tensor(W[0:8, 16:17], W[0:8, 4:5], W[0:8, 5:6], Op.add))
            V(v.tensor_tensor(W[0:8, 14:15], W[0:8, 8:9], W[0:8, 4:5], Op.mult))
            n = V(v.tensor_scalar(W[0:8, 15:16], W[0:8, 10:11], W[0:8, 5:6], W[0:8, 9:10], Op.mult, Op.add))
            V(v.tensor_scalar(W[0:8, 18:19], W[0:8, ii:ii + 1], 256.0, T.li[0:8, 8:9], Op.mult, Op.add))
            vw(n)
            V(v.tensor_scalar(W[0:8, 17:18], W[0:8, 16:17], -256.0, -256.0, Op.mult, Op.add))
            V(v.tensor_scalar(W[0:8, 20:21], W[0:8, 15:16], W[0:8, 14:15], None, Op.is_gt))
            vw()
            V(v.tensor_scalar(T.tt[0:8, 0:1], W[0:8, 20:21], W[0:8, 17:18], W[0:8, 18:19], Op.mult, Op.add))
        vw()
        n = V(v.transpose(T.tr[0:32, :], T.tt[0:32, :]))
        g.wait_ge(S.vs, n)
        n = G(g.partition_broadcast(T.bj[:], T.tr[0:1, 0:8], 128))
        v.wait_ge(S.gs, n)
        V(v.tensor_scalar(T.jl[:, 0:16:2], T.bj[:], T.pp[:, 0:1], None, Op.add))
        njl = V(v.tensor_scalar(T.jl[:, 1:16:2], T.bj[:], T.pp[:, 1:2], None, Op.add))
        if bound:
            n1, n2_ = pick(0, 512, 1024, T.jl[:], njl, "pa", "hb", chip_there)
            stat[0] = ("pa", 0, n1, n2_)
            g.wait_ge(S.vs, n1)
            put(T.cores[7 - r], "pa", 0, "win", 1024, 256, "x1", False, off)
            g.wait_ge(S.ss, n2_)
            put(T.cores[7 - r], "pa", 0, "win", 1024, 256, "x1", True, off)
        quantise_x()

    def send_x2():
        x = 256 if inner else 768
        n1, n2_ = pick(x, 0, 1024, T.jl[:], njl, "pa", "hb", half_there)
        if inner:
            stat[1] = ("pa", x, n1, n2_)
        for plane, n in ((False, n1), (True, n2_)):
            g.wait_ge(S.ss if plane else S.vs, n)
            put(T.cores[X2_TO[r]], "pa", x, "win", 1280, 256, "x2", plane, off)

    if hand:
        fc = 0 if inner else 512
        for plane in (False, True):
            half_there(g, plane)
            put(T.cores[partner], "hb", fc, "win", fc, 512, "br", plane, on)
        if inner:
            send_x2()

    PR = [pairs(r, t) for t in range(5)]
    COL, e = {}, 4
    for t in (4, 3, 2, 1):
        COL[t] = e
        e += 4 * len(PR[t])
    SIZE = [e, COL[1], COL[2], COL[3], 4]

    def numbers(t):
        hh, f = TI[t]
        a, b = PR[t][0], PR[t][-1] + 1
        to = T.sab[0:8, :, COL[t]:COL[t] + 4 * (b - a)] if t else T.e0[0:8, :, 0:4 * (b - a)]
        if t % 2 == 0:
            V(v.tensor_tensor(to, T.se[0:8, :, hh, a:b, f:f + 4], T.so[0:8, :, hh, a:b, f:f + 4], Op.subtract))
        else:
            V(v.tensor_tensor(to, T.so[0:8, :, hh, a:b, f:f + 4], T.se[0:8, :, hh, a + 1:b + 1, f:f + 4], Op.subtract))

    level = [0] * 8
    need = []
    for t in range(5):
        for k in range(t % 2, 7, 2):
            level[k] = level[k + 1] = max(level[k], level[k + 1])
        if t < 2:
            level[(4 + t) if h == 0 else (3 - t)] = 1 + t
        need.append(level[r])

    def ready(t):
        lv = need[t]
        if hand and t == 0:
            return "pa", "hb", 512 if inner else 0, 1024 if inner else 512, chip_there
        if third and t < 3:
            return "pa", "hb", 0, 1024, half_there
        if outer and t < 2:
            return "pk", "win", 0, 512, chip_there

        def waits(q, plane):
            if bound and t == 1:
                chip_there(q, plane)
            else:
                half_there(q, plane)
            if not outer:
                q.wait_ge(S.cw, ncw[0])
            if mid:
                if lv >= 1:
                    q.wait_ge(sem("x1", plane), nx1)
                if lv >= 2:
                    q.wait_ge(sem("x2", plane), noff)
            elif lv:
                q.wait_ge(sem("rw", plane), 2 * noff)
        if bound and t == 1:
            return "pk", "win", 512, 1280, waits
        return "pk", "win", 0, 1024 + (256 * lv if mid else 512 * lv), waits

    nlist = {}

    def make_lists(t0, t1, k, shift=False):
        v.wait_ge(S.gs, k)
        fr = T.bf[:, 8 * t0:8 * t1]
        o = 2 if shift else 0
        V(v.tensor_scalar(T.lu[:, 16 * t0:16 * t1:2], fr, T.pp[:, o:o + 1], None, Op.add))
        n = V(v.tensor_scalar(T.lu[:, 16 * t0 + 1:16 * t1:2], fr, T.pp[:, o + 1:o + 2], None, Op.add))
        for t in range(t0, t1):
            nlist[t] = n

    def do_pick(t):
        buf, src, wa, wb, waits = ready(t)
        n1, n2_ = pick(256 * t, wa, wb, T.lu[:, 16 * t:16 * t + 16], nlist[t], buf, src, waits)
        stat[t] = (buf, 256 * t, n1, n2_)

    v.wait_ge(S.own, 32)
    v.wait_ge(S.sO, cO[0])
    for t in range(3):
        numbers(t)
    v.wait_ge(S.ow2, 32)
    v.wait_ge(S.sP, cP[0])
    for t in (3, 4):
        numbers(t)

    f0, f1 = (1, 2) if bound else (0, 1) if inner else (0, 2)
    groups = {f1 - 1: (f0, f1), 3: (2, 4), 4: (4, 5)}
    pb, last = {}, cv[0]

    def turn(t):
        if t < f0 or f1 <= t < 2:
            return
        k = V(v.transpose(T.tf[0:32, 8 * t:8 * t + 32], T.sab[0:32, r % 2, m:m + 32]))
        if t in groups:
            a, b = groups[t]
            g.wait_ge(S.vs, k)
            pb[t] = G(g.partition_broadcast(T.bf[0:128, 8 * a:8 * b], T.tf[0:1, 8 * a:8 * b], 128))
            if bound and t < 4:
                plane = t > 1
                g.wait_ge(sem("x1", plane), noff)
                put(T.cores[partner], "win", 1024, "win", 1024, 256, "x1", plane, near)

    for t in range(5):
        n, odd = SIZE[t], t % 2
        n16 = -(-n // 16)
        lo, np = PR[t][0], len(PR[t])
        a, b = (T.sab[0:8, 1, 0:n], T.sab[0:8, 0, 1:n + 1]) if odd else (T.sab[0:8, 0, 0:n], T.sab[0:8, 1, 0:n])
        eb, c = (T.sab, COL[t] + lo) if t else (T.e0, lo)
        w = 5 * np - 4
        ea, eb = eb[0:8, odd, c:c + w:5], eb[0:8, 1 - odd, c + odd:c + odd + w:5]
        cc = T.co if odd else T.ce
        vw(last)
        V(v.tensor_tensor(cc[0:8, lo:lo + np], eb, ea, Op.is_gt))
        k = V(v.tensor_tensor(T.dd[0:8, 0:n], b, a, Op.subtract))
        if t:
            turn(t - 1)
        vw(k)
        of = T.oz if mid and t == 0 else T.of
        k = V(v.tensor_tensor(T.cd[:, 0:16 * n16], cc[:, 0:8].indirect(of[:, 0:n16]), T.dd[:, 0:16 * n16], Op.mult))
        if t == 3:
            make_lists(f0, f1, pb[f1 - 1], mid)
        vw(k)
        V(v.tensor_tensor(a, a, T.cd[0:8, 0:n], Op.add))
        last = V(v.tensor_tensor(b, b, T.cd[0:8, 0:n], Op.subtract))
        if t == 0 and not outer:
            sy.wait_ge(S.vs, last if bound else nq)
            for plane in (False, True):
                (half_there if hand else chip_there)(sy, plane)
            to_win(512 if bound else 0, 512 if bound else 1024)
        if third and t == 2:
            send_x2()
        if t == 3 and not bound:
            do_pick(0)
    vw(last)
    turn(4)

    copied = {}
    VB = (2, 3) if inner else (2,)

    def out(t):
        o = 256 * t
        e = [512 * ((2 * t + k) % 8) for k in range(2)]
        v.wait_ge(S.ps, 2 * t + 1)
        n1 = V(v.tensor_copy(T.ys[:, o:o + 128], T.acc[:, e[0]:e[0] + 128]))
        if t in VB:
            v.wait_ge(S.ps, 2 * t + 2)
            n1 = V(v.tensor_copy(T.ys[:, o + 128:o + 256], T.acc[:, e[1]:e[1] + 128]))
            n2_ = 0
        else:
            sc.wait_ge(S.ps, 2 * t + 2)
            n2_ = A(sc.activation(T.ys[:, o + 128:o + 256], T.acc[:, e[1]:e[1] + 128], Act.Copy))
        copied[t] = (n1, n2_)
        sy.wait_ge(S.vs, n1)
        if t < 4:
            if n2_:
                sy.wait_ge(S.ss, n2_)
            sy.dma_start(T.y[:, o:o + 256], T.ys[:, o:o + 256]).then_inc(S.st, 16)
            cst[0] += 16
        else:
            sy.dma_start(T.y[:, o:o + 128], T.ys[:, o:o + 128]).then_inc(S.st, 16)
            sc.wait_ge(S.ss, n2_)
            sc.dma_start(T.y[:, o + 128:o + 256], T.ys[:, o + 128:o + 256]).then_inc(S.st, 16)
            cst[0] += 32

    def product(t, ks=(0, 1)):
        buf, x, n1, n2_ = stat[t]
        te.wait_ge(S.vs, max(n1, nx[0]))
        te.wait_ge(S.ss, n2_)
        if t == 4:
            te.wait_ge(S.vs, copied[0][0])
            te.wait_ge(S.ss, copied[0][1])
        for k in ks:
            e = 512 * ((2 * t + k) % 8)
            c = x + 128 * k
            te.matmul_mx(T.acc[:, e:e + 128], T[buf][:, c:c + 128], T[buf + "s"][:, c:c + 128],
                         T.xq[:, 128 * t:128 * t + 128], T.xs[:, 128 * t:128 * t + 128], True, True).then_inc(S.ps, 1)

    for t in range(5):
        if inner and t == 2:
            out(1)
        if t in (2, 4):
            make_lists(t, min(5, t + 2), pb[4 if t == 4 else 3])
        if t not in stat and t < 4:
            do_pick(t)
        if t < 4:
            product(t)
        else:
            buf, src, wa, wb, waits = ready(t)
            for k in range(2):
                n1, n2_ = pick(256 * t + 128 * k, wa, wb, T.lu[:, 16 * t + 8 * k:16 * t + 8 * k + 8], nlist[t], buf, src,
                               waits, 128)
                stat[t] = (buf, 256 * t, n1, n2_)
                product(t, (k,))
        if t > 0 and (t != 2 or not inner):
            out(t - 1)
    out(4)

    for plane in (False, True):
        half_there(v, plane)
        for name, n in (("x1", nx1), ("x2", noff)) if mid else (("rw", 2 * noff),):
            v.wait_ge(sem(name, plane), n)
    vw()
    sc.wait_ge(S.ss, cs[0])
    te.wait_ge(S.ps, 10)
    sy.wait_ge(S.st, cst[0])
    g.wait_ge(S.gs, cg[0])
    g.wait_ge(S.ls, cl[0])
